import numpy as np
import ml_dtypes


def mxq(x, axis, fmt="e4m3"):
    dtype, down = {"e4m3": (ml_dtypes.float8_e4m3fn, 7), "e5m2": (ml_dtypes.float8_e5m2, 14)}[fmt]
    v = np.moveaxis(np.asarray(x, np.float32).astype(ml_dtypes.bfloat16).astype(np.float64), axis, -1)
    blocks = v.reshape(v.shape[:-1] + (-1, 32))
    amax = np.abs(blocks).max(-1, keepdims=True)
    byte = np.maximum(np.where(amax > 0, np.frexp(amax)[1] - 1 + 127, 0) - down, 1)
    scale = np.exp2(byte - 127.0)
    codes = (blocks / scale).astype(np.float32).astype(dtype).astype(np.float64)
    return np.moveaxis((codes * scale).reshape(v.shape), -1, axis)


WIDE = False


def mx_kscale(k):
    if not WIDE:
        return np.ones(k)
    levels = np.array([10, -10, 5, -5, 0])
    if k % 512:
        return np.exp2(np.random.permutation(np.resize(levels, k // 32))).repeat(32)
    a = np.empty((k // 512, 16))
    for p in range(k // 512):
        a[p, :8] = np.random.permutation(np.resize(levels, 8))
        for g in range(8):
            far = levels[np.abs(levels - a[p, g]) >= 10]
            a[p, g + 8] = far[np.random.randint(len(far))]
    return np.exp2(a.ravel()).repeat(32)


def f64(x):
    return np.asarray(x).astype(np.float64)


def striped(idx):
    return np.tile(idx.reshape(-1, 16).T, (8, 1)).astype(np.uint16)


def unstriped(offs):
    return offs[:16].T.reshape(-1).astype(np.int64)


def pack_weight(w):
    k, n = w.shape
    w = f64(np.asarray(w, np.float32).astype(ml_dtypes.bfloat16)).reshape(k // 32, 32, n)
    amax = np.abs(w).max(1)
    byte = np.clip(np.where(amax > 0, np.frexp(amax)[1] - 1 + 127 - 7, 1), 1, 254)
    scaled = (w * np.exp2(127.0 - byte)[:, None, :]).reshape(k, n).astype(np.float32)
    words = np.ascontiguousarray(scaled.reshape(k // 512, 128, 4, n).transpose(0, 1, 3, 2)).astype(ml_dtypes.float8_e4m3fn).view(np.uint8)
    return words, np.ascontiguousarray(byte.astype(np.uint8).reshape(k // 512, 16, n))


def unpack_weight(words, scales):
    g, p, n, _ = words.shape
    vals = np.ascontiguousarray(words).view(ml_dtypes.float8_e4m3fn).astype(np.float64) * np.repeat(np.exp2(scales.astype(np.float64) - 127.0), 8, axis=1)[..., None]
    return vals.transpose(0, 1, 3, 2).reshape(g * 512, n)


def planes(y):
    n, m = y.shape
    v = y.astype(np.float32).astype(ml_dtypes.bfloat16).astype(np.float64).reshape(n // 32, 32, m)
    top = np.abs(v).max(1)
    byte = np.clip(np.where(top > 0, np.frexp(top)[1] - 1 + 127 - 7, 1), 1, 254)
    codes = (v * np.exp2(127.0 - byte)[:, None, :]).reshape(n, m).astype(np.float32).astype(ml_dtypes.float8_e4m3fn).view(np.uint8)
    words = codes.reshape(n // 512, 128, 4, m).transpose(0, 1, 3, 2)
    return np.ascontiguousarray(words), np.ascontiguousarray(byte.astype(np.uint8).reshape(n // 512, 16, m))


def sigmoid(v):
    return 1.0 / (1.0 + np.exp(-np.maximum(v, -700.0)))


K, T, S, N, U = 512, 2048, 512, 512, 1024


def setup_inputs():
    n = np.random.standard_normal
    s = mx_kscale(K)[:, None]
    packed_xT = pack_weight(n((K, T)) * s)
    return {
        "x_words": packed_xT[0],
        "x_scales": packed_xT[1],
        "cache": (n((N, U))).astype(np.float32),
        "w1": (n((K, N)) / np.sqrt(K) / s).astype(np.float32),
        "w2": (n((K, N)) / np.sqrt(K) / s).astype(np.float32),
        "offs": striped(np.random.permutation(T)[:S]),
        "slot": striped(np.random.permutation(U)[:S]),
    }


def reference(x_words, x_scales, cache, w1, w2, offs, slot):
    xq = unpack_weight(x_words, x_scales)[:, unstriped(offs)]
    y = mxq(f64(w1), 0, "e4m3").T @ xq
    e = sigmoid(mxq(f64(w2), 0, "e4m3").T @ xq)
    r = y * e
    out = f64(cache).copy()
    out[:, unstriped(slot)] = r
    out_0 = out
    return (out_0,) + planes(out_0)

@@ -1,0 +1,152 @@
+from contextlib import ExitStack
+
+import concourse.mybir as mybir
+
+K, T, S, N, U = 512, 2048, 512, 512, 1024
+FLOPS = 2 * 2 * K * N * S
+
+F32 = mybir.dt.float32
+BF16 = mybir.dt.bfloat16
+I32 = mybir.dt.int32
+U32 = mybir.dt.uint32
+U16 = mybir.dt.uint16
+U8 = mybir.dt.uint8
+FP8X4 = mybir.dt.float8_e4m3fn_x4
+SIGMOID = mybir.ActivationFunctionType.Sigmoid
+MULT = mybir.AluOpType.mult
+
+P = 128
+PACK = 4
+HALF = S // 2
+PIECE = 256
+PIECES = U // PIECE
+VECTOR_PIECES = 2
+ROW_ORDER = (0, 2, 3, 1)
+
+
+def tile_picked_zkvw_two_po_kernel(
+    tc, x_words, x_scales, cache, w1, w2, offs, slot, out_0, out_1, out_2
+):
+    nc = tc.nc
+    with ExitStack() as ctx:
+        sb = ctx.enter_context(tc.tile_pool(name="sb", bufs=1))
+        psum = ctx.enter_context(tc.psum_pool(name="psum", bufs=8))
+
+        offs_sb = sb.tile([P, S // 16], U16, name="offs_sb")
+        slot_sb = sb.tile([P, S // 16], U16, name="slot_sb")
+        word_table = sb.tile([P, T], U32, name="word_table", align_bytes=64)
+        scale_table = sb.tile([P, T], U8, name="scale_table", align_bytes=64)
+        w2_raw = sb.tile([P, PACK, N], F32, name="w2_raw", align_bytes=64)
+        w1_raw = sb.tile([P, PACK, N], F32, name="w1_raw", align_bytes=64)
+        rows = [sb.tile([P, U], F32, name="rows%d" % t, align_bytes=64) for t in range(PACK)]
+
+        warm_in = sb.tile([P, 1], F32, name="warm_in")
+        warm_out = sb.tile([P, 1], F32, name="warm_out")
+        nc.vector.memset(scale_table[:].bitcast(I32), 0)
+        nc.vector.memset(warm_in[:], 0.0)
+        nc.scalar.activation(warm_out[:], warm_in[:], SIGMOID)
+
+        nc.sync.dma_start(offs_sb[:], offs)
+        nc.sync.dma_start(w2_raw[:], w2.rearrange("(p j) c -> p j c", j=PACK))
+        for q in range(4):
+            nc.sync.dma_start(
+                scale_table[32 * q : 32 * q + 4, :].bitcast(I32), x_scales[0, 4 * q : 4 * q + 4, :].bitcast(I32)
+            )
+        nc.sync.dma_start(w1_raw[:], w1.rearrange("(p j) c -> p j c", j=PACK))
+        nc.sync.dma_start(word_table[:].bitcast(I32), x_words[0].rearrange("p n t -> p (n t)").bitcast(I32))
+        nc.sync.dma_start(slot_sb[:], slot)
+        cache_rows = cache.rearrange("(p t) c -> p t c", t=PACK)
+        for t in ROW_ORDER:
+            nc.sync.dma_start(rows[t][:], cache_rows[:, t, :])
+
+        def quantize_weight(raw, label):
+            source = raw[:].rearrange("p j (m t) -> p m j t", t=PACK)
+            dealt = [sb.tile([P, 2 * P * PACK], BF16, name="%s_dealt%d" % (label, u), align_bytes=64) for u in range(2)]
+            views = [d[:].rearrange("p (t m j) -> p m j t", t=2, j=PACK) for d in dealt]
+            nc.vector.tensor_copy(views[0], source[:, :, :, 0:2])
+            nc.scalar.copy(views[1], source[:, :, :, 2:4])
+            operands = []
+            for u in range(2):
+                codes = sb.tile([P, 2 * P], U32, name="%s_codes%d" % (label, u), align_bytes=64)
+                scales = sb.tile([P, 2 * P], U8, name="%s_scales%d" % (label, u), align_bytes=64)
+                nc.vector.quantize_mx(out=codes[:].bitcast(FP8X4), scales=scales[:], in_=dealt[u][:])
+                for e in range(2):
+                    operands.append((codes[:, e * P : (e + 1) * P], scales[:, e * P : (e + 1) * P]))
+            return operands
+
+        x_codes = sb.tile([P, S], U32, name="x_codes", align_bytes=64)
+        x_scale = sb.tile([P, S], U8, name="x_scale", align_bytes=64)
+
+        gate_w = quantize_weight(w2_raw, "w2")
+        nc.vector.tensor_copy(x_scale[:], scale_table[:].indirect(offs_sb[:]))
+        value_w = quantize_weight(w1_raw, "w1")
+        for h in range(2):
+            nc.vector.tensor_copy(
+                x_codes[:, h * HALF : (h + 1) * HALF],
+                word_table[:].indirect(offs_sb[:, h * HALF // 16 : (h + 1) * HALF // 16]),
+            )
+
+        def product(weight, lo, hi):
+            acc = psum.tile([P, hi - lo], F32, name="acc")
+            nc.tensor.matmul_mx(
+                out=acc[:],
+                lhsT=weight[0].bitcast(FP8X4),
+                lhsT_scale=weight[1],
+                rhs=x_codes[:, lo:hi].bitcast(FP8X4),
+                rhs_scale=x_scale[:, lo:hi],
+                start=True,
+                stop=True,
+            )
+            return acc
+
+        gates = [sb.tile([P, S], F32, name="gate%d" % a, align_bytes=64) for a in range(PACK)]
+        values = [sb.tile([P, S], F32, name="value%d" % a, align_bytes=64) for a in range(PACK - 1)]
+        values.append(values[0])
+
+        def gate_factor(a, lo, hi):
+            nc.scalar.activation(gates[a][:, lo:hi], product(gate_w[ROW_ORDER[a]], lo, hi)[:], SIGMOID)
+
+        def value_factor(a, lo, hi):
+            nc.scalar.copy(values[a][:, lo:hi], product(value_w[ROW_ORDER[a]], lo, hi)[:])
+
+        for lo in (0, HALF):
+            gate_factor(0, lo, lo + HALF)
+            value_factor(0, lo, lo + HALF)
+        for a in range(1, PACK):
+            gate_factor(a, 0, S)
+            if a < PACK - 1:
+                value_factor(a, 0, S)
+
+        woven = [sb.tile([P, PIECE, PACK], BF16, name="woven%d" % i, align_bytes=64) for i in range(PIECES)]
+        out_rows = out_0.rearrange("(p t) c -> p t c", t=PACK)
+        for a, t in enumerate(ROW_ORDER):
+            for lo, hi in ((0, HALF), (HALF, S)) if a == 0 else ((0, S),):
+                nc.vector.tensor_tensor(
+                    rows[t][:].indirect(slot_sb[:, lo // 16 : hi // 16]), values[a][:, lo:hi], gates[a][:, lo:hi], MULT
+                )
+            nc.sync.dma_start(out_rows[:, t, :], rows[t][:])
+            for i in range(PIECES):
+                source = rows[t][:, i * PIECE : (i + 1) * PIECE]
+                if a == PACK - 1 and i < VECTOR_PIECES:
+                    nc.vector.tensor_copy(woven[i][:, :, t], source)
+                else:
+                    nc.scalar.copy(woven[i][:, :, t], source)
+            if a == 0:
+                value_factor(PACK - 1, 0, S)
+
+        out_codes = sb.tile([P, U], U32, name="out_codes", align_bytes=64)
+        out_scales = sb.tile([P, U], U8, name="out_scales", align_bytes=64)
+        words_hbm = out_1[0].rearrange("p n t -> p (n t)").bitcast(I32)
+        for i in range(PIECES):
+            cols = slice(i * PIECE, (i + 1) * PIECE)
+            nc.vector.quantize_mx(
+                out=out_codes[:, cols].bitcast(FP8X4),
+                scales=out_scales[:, cols],
+                in_=woven[i][:].rearrange("p c t -> p (c t)"),
+            )
+            if i > 0:
+                first = 0 if i == 1 else i * PIECE
+                nc.sync.dma_start(words_hbm[:, first : cols.stop], out_codes[:, first : cols.stop].bitcast(I32))
+        for q in range(4):
+            queue = nc.scalar if q % 2 else nc.sync
+            queue.dma_start(out_2[0, 4 * q : 4 * q + 4, :].bitcast(I32), out_scales[32 * q : 32 * q + 4, :].bitcast(I32))

@@ -18,9 +18,10 @@ MULT = mybir.AluOpType.mult
 P = 128
 PACK = 4
 HALF = S // 2
+LEAD = 128
 PIECE = 256
 PIECES = U // PIECE
-VECTOR_PIECES = 2
+VECTOR_COLUMNS = 640
 ROW_ORDER = (0, 2, 3, 1)
 
 
@@ -46,12 +47,10 @@ def tile_picked_zkvw_two_po_kernel(
         nc.vector.memset(warm_in[:], 0.0)
         nc.scalar.activation(warm_out[:], warm_in[:], SIGMOID)
 
-        nc.sync.dma_start(offs_sb[:], offs)
         nc.sync.dma_start(w2_raw[:], w2.rearrange("(p j) c -> p j c", j=PACK))
-        for q in range(4):
-            nc.sync.dma_start(
-                scale_table[32 * q : 32 * q + 4, :].bitcast(I32), x_scales[0, 4 * q : 4 * q + 4, :].bitcast(I32)
-            )
+        nc.sync.dma_start(offs_sb[:], offs)
+        for r in range(4):
+            nc.sync.dma_start(scale_table[r:P:32, :].bitcast(I32), x_scales[0, r:16:4, :].bitcast(I32))
         nc.sync.dma_start(w1_raw[:], w1.rearrange("(p j) c -> p j c", j=PACK))
         nc.sync.dma_start(word_table[:].bitcast(I32), x_words[0].rearrange("p n t -> p (n t)").bitcast(I32))
         nc.sync.dma_start(slot_sb[:], slot)
@@ -74,7 +73,7 @@ def tile_picked_zkvw_two_po_kernel(
                     operands.append((codes[:, e * P : (e + 1) * P], scales[:, e * P : (e + 1) * P]))
             return operands
 
-        x_codes = sb.tile([P, S], U32, name="x_codes", align_bytes=64)
+        x_codes = [sb.tile([P, HALF], U32, name="x_codes%d" % h, align_bytes=64) for h in range(2)]
         x_scale = sb.tile([P, S], U8, name="x_scale", align_bytes=64)
 
         gate_w = quantize_weight(w2_raw, "w2")
@@ -82,21 +81,24 @@ def tile_picked_zkvw_two_po_kernel(
         value_w = quantize_weight(w1_raw, "w1")
         for h in range(2):
             nc.vector.tensor_copy(
-                x_codes[:, h * HALF : (h + 1) * HALF],
+                x_codes[h][:],
                 word_table[:].indirect(offs_sb[:, h * HALF // 16 : (h + 1) * HALF // 16]),
             )
 
         def product(weight, lo, hi):
             acc = psum.tile([P, hi - lo], F32, name="acc")
-            nc.tensor.matmul_mx(
-                out=acc[:],
-                lhsT=weight[0].bitcast(FP8X4),
-                lhsT_scale=weight[1],
-                rhs=x_codes[:, lo:hi].bitcast(FP8X4),
-                rhs_scale=x_scale[:, lo:hi],
-                start=True,
-                stop=True,
-            )
+            cuts = [lo] + [HALF] * (lo < HALF < hi) + [hi]
+            for start, stop in zip(cuts, cuts[1:]):
+                h = start // HALF
+                nc.tensor.matmul_mx(
+                    out=acc[:, start - lo : stop - lo],
+                    lhsT=weight[0].bitcast(FP8X4),
+                    lhsT_scale=weight[1],
+                    rhs=x_codes[h][:, start - h * HALF : stop - h * HALF].bitcast(FP8X4),
+                    rhs_scale=x_scale[:, start:stop],
+                    start=True,
+                    stop=True,
+                )
             return acc
 
         gates = [sb.tile([P, S], F32, name="gate%d" % a, align_bytes=64) for a in range(PACK)]
@@ -109,9 +111,9 @@ def tile_picked_zkvw_two_po_kernel(
         def value_factor(a, lo, hi):
             nc.scalar.copy(values[a][:, lo:hi], product(value_w[ROW_ORDER[a]], lo, hi)[:])
 
-        for lo in (0, HALF):
-            gate_factor(0, lo, lo + HALF)
-            value_factor(0, lo, lo + HALF)
+        for lo, hi in ((0, LEAD), (LEAD, S)):
+            gate_factor(0, lo, hi)
+            value_factor(0, lo, hi)
         for a in range(1, PACK):
             gate_factor(a, 0, S)
             if a < PACK - 1:
@@ -120,17 +122,17 @@ def tile_picked_zkvw_two_po_kernel(
         woven = [sb.tile([P, PIECE, PACK], BF16, name="woven%d" % i, align_bytes=64) for i in range(PIECES)]
         out_rows = out_0.rearrange("(p t) c -> p t c", t=PACK)
         for a, t in enumerate(ROW_ORDER):
-            for lo, hi in ((0, HALF), (HALF, S)) if a == 0 else ((0, S),):
+            for lo, hi in ((0, LEAD), (LEAD, S)) if a == 0 else ((0, S),):
                 nc.vector.tensor_tensor(
                     rows[t][:].indirect(slot_sb[:, lo // 16 : hi // 16]), values[a][:, lo:hi], gates[a][:, lo:hi], MULT
                 )
             nc.sync.dma_start(out_rows[:, t, :], rows[t][:])
             for i in range(PIECES):
-                source = rows[t][:, i * PIECE : (i + 1) * PIECE]
-                if a == PACK - 1 and i < VECTOR_PIECES:
-                    nc.vector.tensor_copy(woven[i][:, :, t], source)
-                else:
-                    nc.scalar.copy(woven[i][:, :, t], source)
+                cut = min(max(VECTOR_COLUMNS - i * PIECE, 0), PIECE) if a == PACK - 1 else 0
+                if cut > 0:
+                    nc.vector.tensor_copy(woven[i][:, :cut, t], rows[t][:, i * PIECE : i * PIECE + cut])
+                if cut < PIECE:
+                    nc.scalar.copy(woven[i][:, cut:, t], rows[t][:, i * PIECE + cut : (i + 1) * PIECE])
             if a == 0:
                 value_factor(PACK - 1, 0, S)
 
@@ -147,6 +149,6 @@ def tile_picked_zkvw_two_po_kernel(
             if i > 0:
                 first = 0 if i == 1 else i * PIECE
                 nc.sync.dma_start(words_hbm[:, first : cols.stop], out_codes[:, first : cols.stop].bitcast(I32))
-        for q in range(4):
-            queue = nc.scalar if q % 2 else nc.sync
-            queue.dma_start(out_2[0, 4 * q : 4 * q + 4, :].bitcast(I32), out_scales[32 * q : 32 * q + 4, :].bitcast(I32))
+        for r in range(4):
+            queue = nc.scalar if r % 2 else nc.sync
+            queue.dma_start(out_2[0, r:16:4, :].bitcast(I32), out_scales[r:P:32, :].bitcast(I32))

@@ -41,11 +41,7 @@ def tile_picked_zkvw_two_po_kernel(
         w1_raw = sb.tile([P, PACK, N], F32, name="w1_raw", align_bytes=64)
         rows = [sb.tile([P, U], F32, name="rows%d" % t, align_bytes=64) for t in range(PACK)]
 
-        warm_in = sb.tile([P, 1], F32, name="warm_in")
-        warm_out = sb.tile([P, 1], F32, name="warm_out")
         nc.vector.memset(scale_table[:].bitcast(I32), 0)
-        nc.vector.memset(warm_in[:], 0.0)
-        nc.scalar.activation(warm_out[:], warm_in[:], SIGMOID)
 
         nc.sync.dma_start(w2_raw[:], w2.rearrange("(p j) c -> p j c", j=PACK))
         nc.sync.dma_start(offs_sb[:], offs)

@@ -36,27 +36,22 @@ def tile_picked_zkvw_two_po_kernel(
         offs_sb = sb.tile([P, S // 16], U16, name="offs_sb")
         slot_sb = sb.tile([P, S // 16], U16, name="slot_sb")
         word_table = sb.tile([P, T], U32, name="word_table", align_bytes=64)
-        scale_table = sb.tile([P, T], U8, name="scale_table", align_bytes=64)
+        scale_table = sb.tile([P, T], U8, name="scale_table", tag="after_scales", align_bytes=64)
         w2_raw = sb.tile([P, PACK, N], F32, name="w2_raw", align_bytes=64)
-        w1_raw = sb.tile([P, PACK, N], F32, name="w1_raw", align_bytes=64)
-        rows = [sb.tile([P, U], F32, name="rows%d" % t, align_bytes=64) for t in range(PACK)]
+        w1_raw = sb.tile([P, PACK, N], F32, name="w1_raw", tag="w1_raw", align_bytes=64)
 
         nc.vector.memset(scale_table[:].bitcast(I32), 0)
 
         nc.sync.dma_start(w2_raw[:], w2.rearrange("(p j) c -> p j c", j=PACK))
         nc.sync.dma_start(offs_sb[:], offs)
-        for r in range(4):
-            nc.sync.dma_start(scale_table[r:P:32, :].bitcast(I32), x_scales[0, r:16:4, :].bitcast(I32))
+        nc.sync.dma_start(scale_table[0:P:8, :].bitcast(I32), x_scales[0].bitcast(I32))
         nc.sync.dma_start(w1_raw[:], w1.rearrange("(p j) c -> p j c", j=PACK))
         nc.sync.dma_start(word_table[:].bitcast(I32), x_words[0].rearrange("p n t -> p (n t)").bitcast(I32))
         nc.sync.dma_start(slot_sb[:], slot)
-        cache_rows = cache.rearrange("(p t) c -> p t c", t=PACK)
-        for t in ROW_ORDER:
-            nc.sync.dma_start(rows[t][:], cache_rows[:, t, :])
 
         def quantize_weight(raw, label):
             source = raw[:].rearrange("p j (m t) -> p m j t", t=PACK)
-            dealt = [sb.tile([P, 2 * P * PACK], BF16, name="%s_dealt%d" % (label, u), align_bytes=64) for u in range(2)]
+            dealt = [sb.tile([P, 2 * P * PACK], BF16, name="%s_dealt%d" % (label, u), tag="%s_dealt%d" % (label, u), align_bytes=64) for u in range(2)]
             views = [d[:].rearrange("p (t m j) -> p m j t", t=2, j=PACK) for d in dealt]
             nc.vector.tensor_copy(views[0], source[:, :, :, 0:2])
             nc.scalar.copy(views[1], source[:, :, :, 2:4])
@@ -71,10 +66,19 @@ def tile_picked_zkvw_two_po_kernel(
 
         x_codes = [sb.tile([P, HALF], U32, name="x_codes%d" % h, align_bytes=64) for h in range(2)]
         x_scale = sb.tile([P, S], U8, name="x_scale", align_bytes=64)
+        picked_scales = sb.tile([P, S], U8, name="picked_scales", align_bytes=64)
+        nc.vector.memset(x_scale[:].bitcast(I32), 0)
 
         gate_w = quantize_weight(w2_raw, "w2")
-        nc.vector.tensor_copy(x_scale[:], scale_table[:].indirect(offs_sb[:]))
+        nc.vector.tensor_copy(picked_scales[:], scale_table[:].indirect(offs_sb[:]))
+        for r in range(4):
+            nc.sync.dma_start(x_scale[r:P:32, :].bitcast(I32), picked_scales[8 * r : P : 32, :].bitcast(I32))
         value_w = quantize_weight(w1_raw, "w1")
+        cache_rows = cache.rearrange("(p t) c -> p t c", t=PACK)
+        rows = [None] * PACK
+        for t, tag in zip(ROW_ORDER, ("after_scales", "w1_raw", "w1_dealt0", "w1_dealt1")):
+            rows[t] = sb.tile([P, U], F32, name="rows%d" % t, tag=tag, align_bytes=64)
+            nc.sync.dma_start(rows[t][:], cache_rows[:, t, :])
         for h in range(2):
             nc.vector.tensor_copy(
                 x_codes[h][:],

@@ -19,9 +19,10 @@ P = 128
 PACK = 4
 HALF = S // 2
 LEAD = 128
-PIECE = 256
-PIECES = U // PIECE
-VECTOR_COLUMNS = 640
+LINK = 16
+PIECES = (0, 256, 512, 768, 896, 1024)
+STORES = (0, 512, 896, 1024)
+VECTOR_COLUMNS = 544
 ROW_ORDER = (0, 2, 3, 1)
 
 
@@ -102,8 +103,10 @@ def tile_picked_zkvw_two_po_kernel(
             return acc
 
         gates = [sb.tile([P, S], F32, name="gate%d" % a, align_bytes=64) for a in range(PACK)]
-        values = [sb.tile([P, S], F32, name="value%d" % a, align_bytes=64) for a in range(PACK - 1)]
-        values.append(values[0])
+        first_and_last = sb.tile([P, 2 * S - LINK], F32, name="first_and_last", align_bytes=64)
+        middle = [sb.tile([P, S], F32, name="value%d" % a, align_bytes=64) for a in (1, 2)]
+        values = [first_and_last[:, S - LINK :], middle[0][:], middle[1][:], first_and_last[:, :S]]
+        last_bank = []
 
         def gate_factor(a, lo, hi):
             nc.scalar.activation(gates[a][:, lo:hi], product(gate_w[ROW_ORDER[a]], lo, hi)[:], SIGMOID)
@@ -118,8 +121,12 @@ def tile_picked_zkvw_two_po_kernel(
             gate_factor(a, 0, S)
             if a < PACK - 1:
                 value_factor(a, 0, S)
+            else:
+                last_bank.append(product(value_w[ROW_ORDER[a]], 0, S))
+                nc.scalar.copy(values[a][:, : S - LINK], last_bank[0][:, : S - LINK])
 
-        woven = [sb.tile([P, PIECE, PACK], BF16, name="woven%d" % i, align_bytes=64) for i in range(PIECES)]
+        woven = sb.tile([P, U * PACK], BF16, name="woven", align_bytes=64)
+        planes = woven[:].rearrange("p (c t) -> p c t", t=PACK)
         out_rows = out_0.rearrange("(p t) c -> p t c", t=PACK)
         for a, t in enumerate(ROW_ORDER):
             for lo, hi in ((0, LEAD), (LEAD, S)) if a == 0 else ((0, S),):
@@ -127,28 +134,31 @@ def tile_picked_zkvw_two_po_kernel(
                     rows[t][:].indirect(slot_sb[:, lo // 16 : hi // 16]), values[a][:, lo:hi], gates[a][:, lo:hi], MULT
                 )
             nc.sync.dma_start(out_rows[:, t, :], rows[t][:])
-            for i in range(PIECES):
-                cut = min(max(VECTOR_COLUMNS - i * PIECE, 0), PIECE) if a == PACK - 1 else 0
-                if cut > 0:
-                    nc.vector.tensor_copy(woven[i][:, :cut, t], rows[t][:, i * PIECE : i * PIECE + cut])
-                if cut < PIECE:
-                    nc.scalar.copy(woven[i][:, cut:, t], rows[t][:, i * PIECE + cut : (i + 1) * PIECE])
+            if a < PACK - 1:
+                nc.scalar.copy(planes[:, :, t], rows[t][:])
+            else:
+                for lo, hi in ((0, 256), (256, VECTOR_COLUMNS)):
+                    nc.vector.tensor_copy(planes[:, lo:hi, t], rows[t][:, lo:hi])
+                for lo, hi in ((VECTOR_COLUMNS, 768), (768, 896), (896, U)):
+                    nc.scalar.copy(planes[:, lo:hi, t], rows[t][:, lo:hi])
             if a == 0:
-                value_factor(PACK - 1, 0, S)
+                nc.scalar.copy(values[PACK - 1][:, S - LINK :], last_bank[0][:, S - LINK :])
 
         out_codes = sb.tile([P, U], U32, name="out_codes", align_bytes=64)
-        out_scales = sb.tile([P, U], U8, name="out_scales", align_bytes=64)
+        out_scales = sb.tile([P, U // 2], U8, name="out_scales", align_bytes=64)
         words_hbm = out_1[0].rearrange("p n t -> p (n t)").bitcast(I32)
-        for i in range(PIECES):
-            cols = slice(i * PIECE, (i + 1) * PIECE)
+        for lo, hi in zip(PIECES, PIECES[1:]):
             nc.vector.quantize_mx(
-                out=out_codes[:, cols].bitcast(FP8X4),
-                scales=out_scales[:, cols],
-                in_=woven[i][:].rearrange("p c t -> p (c t)"),
+                out=out_codes[:, lo:hi].bitcast(FP8X4),
+                scales=out_scales[4 * (lo // S) :, lo % S : lo % S + hi - lo],
+                in_=woven[:, lo * PACK : hi * PACK],
             )
-            if i > 0:
-                first = 0 if i == 1 else i * PIECE
-                nc.sync.dma_start(words_hbm[:, first : cols.stop], out_codes[:, first : cols.stop].bitcast(I32))
-        for r in range(4):
-            queue = nc.scalar if r % 2 else nc.sync
-            queue.dma_start(out_2[0, r:16:4, :].bitcast(I32), out_scales[r:P:32, :].bitcast(I32))
+            if hi in STORES:
+                first = STORES[STORES.index(hi) - 1]
+                nc.sync.dma_start(words_hbm[:, first:hi], out_codes[:, first:hi].bitcast(I32))
+        for q in range(4):
+            queue = nc.scalar if q % 2 else nc.sync
+            queue.dma_start(
+                out_2[0, 4 * q : 4 * q + 4, :].rearrange("r (h c) -> h r c", h=2).bitcast(I32),
+                out_scales[32 * q : 32 * q + 8, :].bitcast(I32),
+            )

@@ -22,7 +22,7 @@ LEAD = 128
 LINK = 16
 PIECES = (0, 256, 512, 768, 896, 1024)
 STORES = (0, 512, 896, 1024)
-VECTOR_COLUMNS = 544
+VECTOR_COLUMNS = 512
 ROW_ORDER = (0, 2, 3, 1)
 
 
@@ -56,25 +56,35 @@ def tile_picked_zkvw_two_po_kernel(
             views = [d[:].rearrange("p (t m j) -> p m j t", t=2, j=PACK) for d in dealt]
             nc.vector.tensor_copy(views[0], source[:, :, :, 0:2])
             nc.scalar.copy(views[1], source[:, :, :, 2:4])
-            operands = []
+            codes = sb.tile([P, N], U32, name="%s_codes" % label, align_bytes=64)
+            scales = sb.tile([P, N], U8, name="%s_scales" % label, align_bytes=64)
             for u in range(2):
-                codes = sb.tile([P, 2 * P], U32, name="%s_codes%d" % (label, u), align_bytes=64)
-                scales = sb.tile([P, 2 * P], U8, name="%s_scales%d" % (label, u), align_bytes=64)
-                nc.vector.quantize_mx(out=codes[:].bitcast(FP8X4), scales=scales[:], in_=dealt[u][:])
-                for e in range(2):
-                    operands.append((codes[:, e * P : (e + 1) * P], scales[:, e * P : (e + 1) * P]))
-            return operands
+                cols = slice(2 * P * u, 2 * P * (u + 1))
+                nc.vector.quantize_mx(out=codes[:, cols].bitcast(FP8X4), scales=scales[:, cols], in_=dealt[u][:])
+            operands = [(codes[:, t * P : (t + 1) * P], scales[:, t * P : (t + 1) * P]) for t in range(PACK)]
+            return operands, codes, scales
 
         x_codes = [sb.tile([P, HALF], U32, name="x_codes%d" % h, align_bytes=64) for h in range(2)]
         x_scale = sb.tile([P, S], U8, name="x_scale", align_bytes=64)
         picked_scales = sb.tile([P, S], U8, name="picked_scales", align_bytes=64)
         nc.vector.memset(x_scale[:].bitcast(I32), 0)
 
-        gate_w = quantize_weight(w2_raw, "w2")
+        gate_w, gate_codes, gate_scales = quantize_weight(w2_raw, "w2")
         nc.vector.tensor_copy(picked_scales[:], scale_table[:].indirect(offs_sb[:]))
         for r in range(4):
             nc.sync.dma_start(x_scale[r:P:32, :].bitcast(I32), picked_scales[8 * r : P : 32, :].bitcast(I32))
-        value_w = quantize_weight(w1_raw, "w1")
+        value_w = quantize_weight(w1_raw, "w1")[0]
+        warm = psum.tile([P, S], F32, name="acc")
+        for turn in range(2):
+            nc.tensor.matmul_mx(
+                out=warm[:],
+                lhsT=value_w[turn][0].bitcast(FP8X4),
+                lhsT_scale=value_w[turn][1],
+                rhs=gate_codes[:].bitcast(FP8X4),
+                rhs_scale=gate_scales[:],
+                start=True,
+                stop=True,
+            )
         cache_rows = cache.rearrange("(p t) c -> p t c", t=PACK)
         rows = [None] * PACK
         for t, tag in zip(ROW_ORDER, ("after_scales", "w1_raw", "w1_dealt0", "w1_dealt1")):
@@ -114,9 +124,11 @@ def tile_picked_zkvw_two_po_kernel(
         def value_factor(a, lo, hi):
             nc.scalar.copy(values[a][:, lo:hi], product(value_w[ROW_ORDER[a]], lo, hi)[:])
 
-        for lo, hi in ((0, LEAD), (LEAD, S)):
-            gate_factor(0, lo, hi)
-            value_factor(0, lo, hi)
+        gate_factor(0, 0, LEAD)
+        value_factor(0, 0, LEAD)
+        value_factor(0, LEAD, HALF)
+        gate_factor(0, LEAD, S)
+        value_factor(0, HALF, S)
         for a in range(1, PACK):
             gate_factor(a, 0, S)
             if a < PACK - 1:

@@ -50,6 +50,9 @@ def tile_picked_zkvw_two_po_kernel(
         nc.sync.dma_start(word_table[:].bitcast(I32), x_words[0].rearrange("p n t -> p (n t)").bitcast(I32))
         nc.sync.dma_start(slot_sb[:], slot)
 
+        table_warm = sb.tile([P, 1], F32, name="table_warm")
+        nc.scalar.activation(table_warm[:], w2_raw[:, 0, 0:1], SIGMOID)
+
         def quantize_weight(raw, label):
             source = raw[:].rearrange("p j (m t) -> p m j t", t=PACK)
             dealt = [sb.tile([P, 2 * P * PACK], BF16, name="%s_dealt%d" % (label, u), tag="%s_dealt%d" % (label, u), align_bytes=64) for u in range(2)]
@@ -98,8 +101,9 @@ def tile_picked_zkvw_two_po_kernel(
 
         def product(weight, lo, hi):
             acc = psum.tile([P, hi - lo], F32, name="acc")
-            cuts = [lo] + [HALF] * (lo < HALF < hi) + [hi]
-            for start, stop in zip(cuts, cuts[1:]):
+            width = HALF if hi - lo == S else LEAD
+            for start in range(lo, hi, width):
+                stop = start + width
                 h = start // HALF
                 nc.tensor.matmul_mx(
                     out=acc[:, start - lo : stop - lo],

@@ -18,12 +18,11 @@ MULT = mybir.AluOpType.mult
 P = 128
 PACK = 4
 HALF = S // 2
-LEAD = 128
-LINK = 16
+COPY = mybir.ActivationFunctionType.Copy
+ADD = mybir.AluOpType.add
 PIECES = (0, 256, 512, 768, 896, 1024)
 STORES = (0, 512, 896, 1024)
-VECTOR_COLUMNS = 512
-ROW_ORDER = (0, 2, 3, 1)
+SPLIT = 512
 
 
 def tile_picked_zkvw_two_po_kernel(
@@ -90,7 +89,7 @@ def tile_picked_zkvw_two_po_kernel(
             )
         cache_rows = cache.rearrange("(p t) c -> p t c", t=PACK)
         rows = [None] * PACK
-        for t, tag in zip(ROW_ORDER, ("after_scales", "w1_raw", "w1_dealt0", "w1_dealt1")):
+        for t, tag in zip((1, 0, 3, 2), ("after_scales", "w1_raw", "w1_dealt0", "w1_dealt1")):
             rows[t] = sb.tile([P, U], F32, name="rows%d" % t, tag=tag, align_bytes=64)
             nc.sync.dma_start(rows[t][:], cache_rows[:, t, :])
         for h in range(2):
@@ -99,75 +98,69 @@ def tile_picked_zkvw_two_po_kernel(
                 word_table[:].indirect(offs_sb[:, h * HALF // 16 : (h + 1) * HALF // 16]),
             )
 
-        def product(weight, lo, hi):
-            acc = psum.tile([P, hi - lo], F32, name="acc")
-            width = HALF if hi - lo == S else LEAD
-            for start in range(lo, hi, width):
-                stop = start + width
-                h = start // HALF
+        def product(weights, h):
+            acc = psum.tile([P, 2, HALF], F32, name="acc")
+            for e in range(2):
                 nc.tensor.matmul_mx(
-                    out=acc[:, start - lo : stop - lo],
-                    lhsT=weight[0].bitcast(FP8X4),
-                    lhsT_scale=weight[1],
-                    rhs=x_codes[h][:, start - h * HALF : stop - h * HALF].bitcast(FP8X4),
-                    rhs_scale=x_scale[:, start:stop],
+                    out=acc[:, e, :],
+                    lhsT=weights[e][0].bitcast(FP8X4),
+                    lhsT_scale=weights[e][1],
+                    rhs=x_codes[h][:].bitcast(FP8X4),
+                    rhs_scale=x_scale[:, h * HALF : (h + 1) * HALF],
                     start=True,
                     stop=True,
                 )
             return acc
 
-        gates = [sb.tile([P, S], F32, name="gate%d" % a, align_bytes=64) for a in range(PACK)]
-        first_and_last = sb.tile([P, 2 * S - LINK], F32, name="first_and_last", align_bytes=64)
-        middle = [sb.tile([P, S], F32, name="value%d" % a, align_bytes=64) for a in (1, 2)]
-        values = [first_and_last[:, S - LINK :], middle[0][:], middle[1][:], first_and_last[:, :S]]
-        last_bank = []
-
-        def gate_factor(a, lo, hi):
-            nc.scalar.activation(gates[a][:, lo:hi], product(gate_w[ROW_ORDER[a]], lo, hi)[:], SIGMOID)
-
-        def value_factor(a, lo, hi):
-            nc.scalar.copy(values[a][:, lo:hi], product(value_w[ROW_ORDER[a]], lo, hi)[:])
-
-        gate_factor(0, 0, LEAD)
-        value_factor(0, 0, LEAD)
-        value_factor(0, LEAD, HALF)
-        gate_factor(0, LEAD, S)
-        value_factor(0, HALF, S)
-        for a in range(1, PACK):
-            gate_factor(a, 0, S)
-            if a < PACK - 1:
-                value_factor(a, 0, S)
-            else:
-                last_bank.append(product(value_w[ROW_ORDER[a]], 0, S))
-                nc.scalar.copy(values[a][:, : S - LINK], last_bank[0][:, : S - LINK])
-
-        woven = sb.tile([P, U * PACK], BF16, name="woven", align_bytes=64)
-        planes = woven[:].rearrange("p (c t) -> p c t", t=PACK)
-        out_rows = out_0.rearrange("(p t) c -> p t c", t=PACK)
-        for a, t in enumerate(ROW_ORDER):
-            for lo, hi in ((0, LEAD), (LEAD, S)) if a == 0 else ((0, S),):
+        rest = U - SPLIT
+        upper = SPLIT + max(S, SPLIT)
+        pitch = upper + rest - SPLIT
+        early = sb.tile([P, 2, S], F32, name="early", align_bytes=64)
+        late = sb.tile([P, SPLIT + 2 * pitch], F32, name="late", align_bytes=64)
+        gated = [early[:], late[:, SPLIT:].rearrange("p (e k) -> p e k", e=2)[:, :, :S]]
+        for u in range(2):
+            for h in range(2):
+                gate = sb.tile([P, 2, HALF], F32, name="gate%d%d" % (u, h), align_bytes=64)
+                nc.scalar.activation(gate[:], product(gate_w[2 * u : 2 * u + 2], h)[:], SIGMOID)
                 nc.vector.tensor_tensor(
-                    rows[t][:].indirect(slot_sb[:, lo // 16 : hi // 16]), values[a][:, lo:hi], gates[a][:, lo:hi], MULT
+                    gated[u][:, :, h * HALF : (h + 1) * HALF], product(value_w[2 * u : 2 * u + 2], h)[:], gate[:], MULT
                 )
-            nc.sync.dma_start(out_rows[:, t, :], rows[t][:])
-            if a < PACK - 1:
-                nc.scalar.copy(planes[:, :, t], rows[t][:])
-            else:
-                for lo, hi in ((0, 256), (256, VECTOR_COLUMNS)):
-                    nc.vector.tensor_copy(planes[:, lo:hi, t], rows[t][:, lo:hi])
-                for lo, hi in ((VECTOR_COLUMNS, 768), (768, 896), (896, U)):
-                    nc.scalar.copy(planes[:, lo:hi, t], rows[t][:, lo:hi])
-            if a == 0:
-                nc.scalar.copy(values[PACK - 1][:, S - LINK :], last_bank[0][:, S - LINK :])
 
+        out_rows = out_0.rearrange("(p t) c -> p t c", t=PACK)
+        spans = ((0, SPLIT), (SPLIT, U))
+        words = [late[:, at : at + 2 * (hi - lo)] for at, (lo, hi) in zip((0, upper), spans)]
+        pairs = [w.bitcast(BF16).rearrange("p (u c e) -> p u c e", u=2, e=2) for w in words]
+        for u in range(2):
+            nc.vector.tensor_copy(rows[2 * u][:].indirect(slot_sb[:]), gated[u][:, 0, :])
+            for h in range(2):
+                nc.scalar.activation(
+                    rows[2 * u + 1][:].indirect(slot_sb[:, h * HALF // 16 : (h + 1) * HALF // 16]),
+                    gated[u][:, 1, h * HALF : (h + 1) * HALF],
+                    COPY,
+                )
+            for e in (1, 0):
+                nc.sync.dma_start(out_rows[:, 2 * u + e, :], rows[2 * u + e][:])
+        for e in (1, 0):
+            for pair, (lo, hi) in zip(pairs, spans):
+                nc.gpsimd.tensor_scalar(pair[:, 0, :, e], rows[e][:, lo:hi], 1.0, -0.0, MULT, ADD)
+        for e in range(2):
+            nc.vector.tensor_copy(pairs[0][:, 1, :, e], rows[2 + e][:, :SPLIT])
+            nc.scalar.copy(pairs[1][:, 1, :, e], rows[2 + e][:, SPLIT:])
+
+        woven = sb.tile([P, U * 2], U32, name="woven", align_bytes=64)
         out_codes = sb.tile([P, U], U32, name="out_codes", align_bytes=64)
         out_scales = sb.tile([P, U // 2], U8, name="out_scales", align_bytes=64)
         words_hbm = out_1[0].rearrange("p n t -> p (n t)").bitcast(I32)
+        words = [w.bitcast(U32).rearrange("p (u c) -> p c u", u=2) for w in words]
+        woven_words = woven[:].rearrange("p (c u) -> p c u", u=2)
+        nc.vector.tensor_copy(woven_words[:, :SPLIT, :].bitcast(I32), words[0].bitcast(I32))
+        for lo, hi in ((SPLIT, 768), (768, 896), (896, U)):
+            nc.scalar.copy(woven_words[:, lo:hi, :], words[1][:, lo - SPLIT : hi - SPLIT, :])
         for lo, hi in zip(PIECES, PIECES[1:]):
             nc.vector.quantize_mx(
                 out=out_codes[:, lo:hi].bitcast(FP8X4),
                 scales=out_scales[4 * (lo // S) :, lo % S : lo % S + hi - lo],
-                in_=woven[:, lo * PACK : hi * PACK],
+                in_=woven[:, lo * 2 : hi * 2].bitcast(BF16),
             )
             if hi in STORES:
                 first = STORES[STORES.index(hi) - 1]

@@ -36,102 +36,86 @@ def tile_picked_zkvw_two_po_kernel(
         offs_sb = sb.tile([P, S // 16], U16, name="offs_sb")
         slot_sb = sb.tile([P, S // 16], U16, name="slot_sb")
         word_table = sb.tile([P, T], U32, name="word_table", align_bytes=64)
-        scale_table = sb.tile([P, T], U8, name="scale_table", tag="after_scales", align_bytes=64)
+        scale_table = sb.tile([P, T], U8, name="scale_table", align_bytes=64)
         w2_raw = sb.tile([P, PACK, N], F32, name="w2_raw", align_bytes=64)
-        w1_raw = sb.tile([P, PACK, N], F32, name="w1_raw", tag="w1_raw", align_bytes=64)
+        w1_raw = sb.tile([P, PACK, N], F32, name="w1_raw", align_bytes=64)
+        rows = [sb.tile([P, U], F32, name="rows%d" % t, align_bytes=64) for t in range(PACK)]
 
         nc.vector.memset(scale_table[:].bitcast(I32), 0)
 
         nc.sync.dma_start(w2_raw[:], w2.rearrange("(p j) c -> p j c", j=PACK))
         nc.sync.dma_start(offs_sb[:], offs)
-        nc.sync.dma_start(scale_table[0:P:8, :].bitcast(I32), x_scales[0].bitcast(I32))
-        nc.sync.dma_start(w1_raw[:], w1.rearrange("(p j) c -> p j c", j=PACK))
+        for q in range(4):
+            nc.sync.dma_start(scale_table[32 * q : 32 * q + 4, :].bitcast(I32), x_scales[0, 4 * q : 4 * q + 4, :].bitcast(I32))
         nc.sync.dma_start(word_table[:].bitcast(I32), x_words[0].rearrange("p n t -> p (n t)").bitcast(I32))
+        nc.sync.dma_start(w1_raw[:], w1.rearrange("(p j) c -> p j c", j=PACK))
         nc.sync.dma_start(slot_sb[:], slot)
+        cache_rows = cache.rearrange("(p t) c -> p t c", t=PACK)
+        for t in (1, 0, 3, 2):
+            nc.sync.dma_start(rows[t][:], cache_rows[:, t, :])
 
-        table_warm = sb.tile([P, 1], F32, name="table_warm")
-        nc.scalar.activation(table_warm[:], w2_raw[:, 0, 0:1], SIGMOID)
-
-        def quantize_weight(raw, label):
+        def quantize_weight(raw, label, second_copy):
             source = raw[:].rearrange("p j (m t) -> p m j t", t=PACK)
-            dealt = [sb.tile([P, 2 * P * PACK], BF16, name="%s_dealt%d" % (label, u), tag="%s_dealt%d" % (label, u), align_bytes=64) for u in range(2)]
+            dealt = [sb.tile([P, 2 * P * PACK], BF16, name="%s_dealt%d" % (label, u), align_bytes=64) for u in range(2)]
             views = [d[:].rearrange("p (t m j) -> p m j t", t=2, j=PACK) for d in dealt]
             nc.vector.tensor_copy(views[0], source[:, :, :, 0:2])
-            nc.scalar.copy(views[1], source[:, :, :, 2:4])
+            second_copy(views[1], source[:, :, :, 2:4])
             codes = sb.tile([P, N], U32, name="%s_codes" % label, align_bytes=64)
             scales = sb.tile([P, N], U8, name="%s_scales" % label, align_bytes=64)
             for u in range(2):
                 cols = slice(2 * P * u, 2 * P * (u + 1))
                 nc.vector.quantize_mx(out=codes[:, cols].bitcast(FP8X4), scales=scales[:, cols], in_=dealt[u][:])
-            operands = [(codes[:, t * P : (t + 1) * P], scales[:, t * P : (t + 1) * P]) for t in range(PACK)]
-            return operands, codes, scales
+            return [(codes[:, t * P : (t + 1) * P], scales[:, t * P : (t + 1) * P]) for t in range(PACK)]
 
-        x_codes = [sb.tile([P, HALF], U32, name="x_codes%d" % h, align_bytes=64) for h in range(2)]
+        x_codes = sb.tile([P, S], U32, name="x_codes", align_bytes=64)
         x_scale = sb.tile([P, S], U8, name="x_scale", align_bytes=64)
-        picked_scales = sb.tile([P, S], U8, name="picked_scales", align_bytes=64)
-        nc.vector.memset(x_scale[:].bitcast(I32), 0)
 
-        gate_w, gate_codes, gate_scales = quantize_weight(w2_raw, "w2")
-        nc.vector.tensor_copy(picked_scales[:], scale_table[:].indirect(offs_sb[:]))
-        for r in range(4):
-            nc.sync.dma_start(x_scale[r:P:32, :].bitcast(I32), picked_scales[8 * r : P : 32, :].bitcast(I32))
-        value_w = quantize_weight(w1_raw, "w1")[0]
-        warm = psum.tile([P, S], F32, name="acc")
-        for turn in range(2):
-            nc.tensor.matmul_mx(
-                out=warm[:],
-                lhsT=value_w[turn][0].bitcast(FP8X4),
-                lhsT_scale=value_w[turn][1],
-                rhs=gate_codes[:].bitcast(FP8X4),
-                rhs_scale=gate_scales[:],
-                start=True,
-                stop=True,
-            )
-        cache_rows = cache.rearrange("(p t) c -> p t c", t=PACK)
-        rows = [None] * PACK
-        for t, tag in zip((1, 0, 3, 2), ("after_scales", "w1_raw", "w1_dealt0", "w1_dealt1")):
-            rows[t] = sb.tile([P, U], F32, name="rows%d" % t, tag=tag, align_bytes=64)
-            nc.sync.dma_start(rows[t][:], cache_rows[:, t, :])
+        gate_w = quantize_weight(w2_raw, "w2", nc.scalar.copy)
+        nc.vector.tensor_copy(x_scale[:], scale_table[:].indirect(offs_sb[:]))
         for h in range(2):
             nc.vector.tensor_copy(
-                x_codes[h][:],
+                x_codes[:, h * HALF : (h + 1) * HALF],
                 word_table[:].indirect(offs_sb[:, h * HALF // 16 : (h + 1) * HALF // 16]),
             )
 
-        def product(weights, h):
-            acc = psum.tile([P, 2, HALF], F32, name="acc")
-            for e in range(2):
+        def product(weights, lo, hi):
+            acc = psum.tile([P, len(weights), hi - lo], F32, name="acc")
+            for e, (codes, scales) in enumerate(weights):
                 nc.tensor.matmul_mx(
                     out=acc[:, e, :],
-                    lhsT=weights[e][0].bitcast(FP8X4),
-                    lhsT_scale=weights[e][1],
-                    rhs=x_codes[h][:].bitcast(FP8X4),
-                    rhs_scale=x_scale[:, h * HALF : (h + 1) * HALF],
+                    lhsT=codes.bitcast(FP8X4),
+                    lhsT_scale=scales,
+                    rhs=x_codes[:, lo:hi].bitcast(FP8X4),
+                    rhs_scale=x_scale[:, lo:hi],
                     start=True,
                     stop=True,
                 )
             return acc
 
-        rest = U - SPLIT
-        upper = SPLIT + max(S, SPLIT)
-        pitch = upper + rest - SPLIT
+        gates = sb.tile([P, PACK, S], F32, name="gates", align_bytes=64)
+        for h in range(2):
+            for u in range(2):
+                lo, hi = h * HALF, (h + 1) * HALF
+                nc.scalar.activation(gates[:, 2 * u : 2 * u + 2, lo:hi], product(gate_w[2 * u : 2 * u + 2], lo, hi)[:], SIGMOID)
+        value_w = quantize_weight(w1_raw, "w1", nc.vector.tensor_copy)
+
         early = sb.tile([P, 2, S], F32, name="early", align_bytes=64)
-        late = sb.tile([P, SPLIT + 2 * pitch], F32, name="late", align_bytes=64)
-        gated = [early[:], late[:, SPLIT:].rearrange("p (e k) -> p e k", e=2)[:, :, :S]]
-        for u in range(2):
-            for h in range(2):
-                gate = sb.tile([P, 2, HALF], F32, name="gate%d%d" % (u, h), align_bytes=64)
-                nc.scalar.activation(gate[:], product(gate_w[2 * u : 2 * u + 2], h)[:], SIGMOID)
-                nc.vector.tensor_tensor(
-                    gated[u][:, :, h * HALF : (h + 1) * HALF], product(value_w[2 * u : 2 * u + 2], h)[:], gate[:], MULT
-                )
+        late = sb.tile([P, 2 * U], F32, name="late", align_bytes=64)
+        gated = [early[:], late[:, U:].rearrange("p (e k) -> p e k", e=2)]
+        for t in (1, 0, 3, 2):
+            acc = product(value_w[t : t + 1], 0, S)
+            if t == 0:
+                nc.scalar.copy(gated[0][:, 0, :], acc[:, 0, :])
+            else:
+                nc.vector.tensor_tensor(gated[t // 2][:, t % 2, :], acc[:, 0, :], gates[:, t, :], MULT)
 
         out_rows = out_0.rearrange("(p t) c -> p t c", t=PACK)
-        spans = ((0, SPLIT), (SPLIT, U))
-        words = [late[:, at : at + 2 * (hi - lo)] for at, (lo, hi) in zip((0, upper), spans)]
-        pairs = [w.bitcast(BF16).rearrange("p (u c e) -> p u c e", u=2, e=2) for w in words]
+        pairs = late[:].bitcast(BF16).rearrange("p (u c e) -> p u c e", u=2, e=2)
         for u in range(2):
-            nc.vector.tensor_copy(rows[2 * u][:].indirect(slot_sb[:]), gated[u][:, 0, :])
+            if u == 0:
+                nc.vector.tensor_tensor(rows[0][:].indirect(slot_sb[:]), gated[0][:, 0, :], gates[:, 0, :], MULT)
+            else:
+                nc.vector.tensor_copy(rows[2][:].indirect(slot_sb[:]), gated[1][:, 0, :])
             for h in range(2):
                 nc.scalar.activation(
                     rows[2 * u + 1][:].indirect(slot_sb[:, h * HALF // 16 : (h + 1) * HALF // 16]),
@@ -141,21 +125,24 @@ def tile_picked_zkvw_two_po_kernel(
             for e in (1, 0):
                 nc.sync.dma_start(out_rows[:, 2 * u + e, :], rows[2 * u + e][:])
         for e in (1, 0):
-            for pair, (lo, hi) in zip(pairs, spans):
-                nc.gpsimd.tensor_scalar(pair[:, 0, :, e], rows[e][:, lo:hi], 1.0, -0.0, MULT, ADD)
-        for e in range(2):
-            nc.vector.tensor_copy(pairs[0][:, 1, :, e], rows[2 + e][:, :SPLIT])
-            nc.scalar.copy(pairs[1][:, 1, :, e], rows[2 + e][:, SPLIT:])
+            nc.gpsimd.tensor_scalar(pairs[:, 0, :, e], rows[e][:], 1.0, -0.0, MULT, ADD)
+        nc.vector.tensor_copy(pairs[:, 1, :SPLIT, 0], rows[2][:, :SPLIT])
+        for lo, hi in ((0, 256), (256, SPLIT)):
+            nc.vector.tensor_copy(pairs[:, 1, lo:hi, 1], rows[3][:, lo:hi])
+        nc.scalar.copy(pairs[:, 1, SPLIT:, 1], rows[3][:, SPLIT:])
+        for lo, hi in ((SPLIT, 768), (768, U)):
+            nc.scalar.copy(pairs[:, 1, lo:hi, 0], rows[2][:, lo:hi])
 
         woven = sb.tile([P, U * 2], U32, name="woven", align_bytes=64)
         out_codes = sb.tile([P, U], U32, name="out_codes", align_bytes=64)
         out_scales = sb.tile([P, U // 2], U8, name="out_scales", align_bytes=64)
         words_hbm = out_1[0].rearrange("p n t -> p (n t)").bitcast(I32)
-        words = [w.bitcast(U32).rearrange("p (u c) -> p c u", u=2) for w in words]
+        words = late[:].bitcast(U32).rearrange("p (u c) -> p c u", u=2)
         woven_words = woven[:].rearrange("p (c u) -> p c u", u=2)
-        nc.vector.tensor_copy(woven_words[:, :SPLIT, :].bitcast(I32), words[0].bitcast(I32))
+        for lo, hi in ((0, 256), (256, SPLIT)):
+            nc.vector.tensor_copy(woven_words[:, lo:hi, :].bitcast(I32), words[:, lo:hi, :].bitcast(I32))
         for lo, hi in ((SPLIT, 768), (768, 896), (896, U)):
-            nc.scalar.copy(woven_words[:, lo:hi, :], words[1][:, lo - SPLIT : hi - SPLIT, :])
+            nc.scalar.copy(woven_words[:, lo:hi, :], words[:, lo:hi, :])
         for lo, hi in zip(PIECES, PIECES[1:]):
             nc.vector.quantize_mx(
                 out=out_codes[:, lo:hi].bitcast(FP8X4),

@@ -37,46 +37,60 @@ def tile_picked_zkvw_two_po_kernel(
         slot_sb = sb.tile([P, S // 16], U16, name="slot_sb")
         word_table = sb.tile([P, T], U32, name="word_table", align_bytes=64)
         scale_table = sb.tile([P, T], U8, name="scale_table", align_bytes=64)
-        w2_raw = sb.tile([P, PACK, N], F32, name="w2_raw", align_bytes=64)
-        w1_raw = sb.tile([P, PACK, N], F32, name="w1_raw", align_bytes=64)
-        rows = [sb.tile([P, U], F32, name="rows%d" % t, align_bytes=64) for t in range(PACK)]
+        w2_raw = [sb.tile([P, 2, N], F32, name="w2_raw%d" % g, align_bytes=64) for g in range(2)]
 
         nc.vector.memset(scale_table[:].bitcast(I32), 0)
 
-        nc.sync.dma_start(w2_raw[:], w2.rearrange("(p j) c -> p j c", j=PACK))
+        w2_rows = w2.rearrange("(p j) c -> p j c", j=PACK)
+        nc.sync.dma_start(w2_raw[0][:], w2_rows[:, 0:2, :])
         nc.sync.dma_start(offs_sb[:], offs)
-        for q in range(4):
-            nc.sync.dma_start(scale_table[32 * q : 32 * q + 4, :].bitcast(I32), x_scales[0, 4 * q : 4 * q + 4, :].bitcast(I32))
+        nc.sync.dma_start(scale_table[0:P:8, :].bitcast(I32), x_scales[0].bitcast(I32))
+        nc.sync.dma_start(w2_raw[1][:], w2_rows[:, 2:4, :])
         nc.sync.dma_start(word_table[:].bitcast(I32), x_words[0].rearrange("p n t -> p (n t)").bitcast(I32))
-        nc.sync.dma_start(w1_raw[:], w1.rearrange("(p j) c -> p j c", j=PACK))
+        w1_rows = w1.rearrange("(p j) c -> p j c", j=PACK)
+        w1_early = sb.tile([P, 2, N], F32, name="w1_early", align_bytes=64)
+        nc.sync.dma_start(w1_early[:], w1_rows[:, 0:2, :])
+        x_codes = sb.tile([P, S], U32, name="x_codes", align_bytes=64)
+        x_scale = sb.tile([P, S], U8, name="x_scale", align_bytes=64)
+        picked_scales = sb.tile([P, S], U8, name="picked_scales", align_bytes=64)
+        nc.vector.memset(x_scale[:].bitcast(I32), 0)
+        nc.vector.tensor_copy(picked_scales[:], scale_table[:].indirect(offs_sb[:]))
+        for r in range(4):
+            nc.sync.dma_start(x_scale[r:P:32, :].bitcast(I32), picked_scales[8 * r : P : 32, :].bitcast(I32))
+        w1_late = sb.tile([P, 2, N], F32, name="w1_late", tag="scale_table", align_bytes=64)
+        nc.sync.dma_start(w1_late[:], w1_rows[:, 2:4, :])
         nc.sync.dma_start(slot_sb[:], slot)
         cache_rows = cache.rearrange("(p t) c -> p t c", t=PACK)
-        for t in (1, 0, 3, 2):
-            nc.sync.dma_start(rows[t][:], cache_rows[:, t, :])
 
-        def quantize_weight(raw, label, second_copy):
-            source = raw[:].rearrange("p j (m t) -> p m j t", t=PACK)
-            dealt = [sb.tile([P, 2 * P * PACK], BF16, name="%s_dealt%d" % (label, u), align_bytes=64) for u in range(2)]
-            views = [d[:].rearrange("p (t m j) -> p m j t", t=2, j=PACK) for d in dealt]
-            nc.vector.tensor_copy(views[0], source[:, :, :, 0:2])
-            second_copy(views[1], source[:, :, :, 2:4])
+        def quantize_weight(dealt, label):
             codes = sb.tile([P, N], U32, name="%s_codes" % label, align_bytes=64)
             scales = sb.tile([P, N], U8, name="%s_scales" % label, align_bytes=64)
             for u in range(2):
                 cols = slice(2 * P * u, 2 * P * (u + 1))
-                nc.vector.quantize_mx(out=codes[:, cols].bitcast(FP8X4), scales=scales[:, cols], in_=dealt[u][:])
+                nc.vector.quantize_mx(out=codes[:, cols].bitcast(FP8X4), scales=scales[:, cols], in_=dealt[u])
             return [(codes[:, t * P : (t + 1) * P], scales[:, t * P : (t + 1) * P]) for t in range(PACK)]
 
-        x_codes = sb.tile([P, S], U32, name="x_codes", align_bytes=64)
-        x_scale = sb.tile([P, S], U8, name="x_scale", align_bytes=64)
+        w2_dealt = sb.tile([P, N * PACK], BF16, name="w2_dealt", align_bytes=64)
+        for g, copy in enumerate((nc.scalar.copy, nc.vector.tensor_copy)):
+            copy(
+                w2_dealt[:].rearrange("p (t m j) -> p m j t", t=PACK, j=PACK)[:, :, 2 * g : 2 * g + 2, :],
+                w2_raw[g][:].rearrange("p j (m t) -> p m j t", t=PACK),
+            )
+        gate_w = quantize_weight([w2_dealt[:, :1024], w2_dealt[:, 1024:]], "w2")
 
-        gate_w = quantize_weight(w2_raw, "w2", nc.scalar.copy)
-        nc.vector.tensor_copy(x_scale[:], scale_table[:].indirect(offs_sb[:]))
+        w1_dealt = sb.tile([P, N * PACK], BF16, name="w1_dealt", align_bytes=64)
+        w1_target = w1_dealt[:].rearrange("p (t m j) -> p m j t", t=PACK, j=PACK)
+        rows = [None] * PACK
+        for t, tag in zip((1, 0, 3, 2), ("w2_raw1", "picked_scales", "word_table", "scale_table")):
+            rows[t] = sb.tile([P, U], F32, name="rows%d" % t, tag=tag, align_bytes=64)
+        for t in (1, 0, 3, 2):
+            nc.sync.dma_start(rows[t][:], cache_rows[:, t, :])
         for h in range(2):
             nc.vector.tensor_copy(
                 x_codes[:, h * HALF : (h + 1) * HALF],
                 word_table[:].indirect(offs_sb[:, h * HALF // 16 : (h + 1) * HALF // 16]),
             )
+        nc.vector.tensor_copy(w1_target[:, :, 0:2, :], w1_early[:].rearrange("p j (m t) -> p m j t", t=PACK))
 
         def product(weights, lo, hi):
             acc = psum.tile([P, len(weights), hi - lo], F32, name="acc")
@@ -94,10 +108,16 @@ def tile_picked_zkvw_two_po_kernel(
 
         gates = sb.tile([P, PACK, S], F32, name="gates", align_bytes=64)
         for h in range(2):
-            for u in range(2):
-                lo, hi = h * HALF, (h + 1) * HALF
-                nc.scalar.activation(gates[:, 2 * u : 2 * u + 2, lo:hi], product(gate_w[2 * u : 2 * u + 2], lo, hi)[:], SIGMOID)
-        value_w = quantize_weight(w1_raw, "w1", nc.vector.tensor_copy)
+            lo, hi = h * HALF, (h + 1) * HALF
+            nc.scalar.activation(gates[:, 0:2, lo:hi], product(gate_w[0:2], lo, hi)[:], SIGMOID)
+        for t in (3, 2):
+            nc.scalar.activation(gates[:, t, :], product(gate_w[t : t + 1], 0, S)[:, 0, :], SIGMOID)
+        for u in range(2):
+            nc.vector.tensor_copy(
+                w1_target[:, :, 2:4, 2 * u : 2 * u + 2],
+                w1_late[:].rearrange("p j (m t) -> p m j t", t=PACK)[:, :, :, 2 * u : 2 * u + 2],
+            )
+        value_w = quantize_weight([w1_dealt[:, :1024], w1_dealt[:, 1024:]], "w1")
 
         early = sb.tile([P, 2, S], F32, name="early", align_bytes=64)
         late = sb.tile([P, 2 * U], F32, name="late", align_bytes=64)

@@ -13,16 +13,21 @@ U16 = mybir.dt.uint16
 U8 = mybir.dt.uint8
 FP8X4 = mybir.dt.float8_e4m3fn_x4
 SIGMOID = mybir.ActivationFunctionType.Sigmoid
+COPY = mybir.ActivationFunctionType.Copy
 MULT = mybir.AluOpType.mult
+ADD = mybir.AluOpType.add
 
 P = 128
 PACK = 4
 HALF = S // 2
-COPY = mybir.ActivationFunctionType.Copy
-ADD = mybir.AluOpType.add
-PIECES = (0, 256, 512, 768, 896, 1024)
-STORES = (0, 512, 896, 1024)
-SPLIT = 512
+LEAD = 128
+PLANE = {1: 0, 3: 1, 0: 2, 2: 3}
+SHARED = 192
+OWN = 384
+ROUNDS = ((384, 640), (0, 384), (640, 1024))
+SCALAR_WEAVES = ((384, 640), (640, 896), (896, 1024))
+QUANTISED = ((384, 512), (0, 256), (256, 384), (512, 768), (768, 896), (896, 1024))
+STORED = {(0, 256): (0, 256), (256, 384): (256, 512), (512, 768): (512, 768), (896, 1024): (768, 1024)}
 
 
 def tile_picked_zkvw_two_po_kernel(
@@ -31,147 +36,177 @@ def tile_picked_zkvw_two_po_kernel(
     nc = tc.nc
     with ExitStack() as ctx:
         sb = ctx.enter_context(tc.tile_pool(name="sb", bufs=1))
-        psum = ctx.enter_context(tc.psum_pool(name="psum", bufs=8))
+        held = ctx.enter_context(tc.tile_pool(name="held", bufs=1))
+        psum = ctx.enter_context(tc.psum_pool(name="psum", bufs=1))
 
         offs_sb = sb.tile([P, S // 16], U16, name="offs_sb")
         slot_sb = sb.tile([P, S // 16], U16, name="slot_sb")
         word_table = sb.tile([P, T], U32, name="word_table", align_bytes=64)
-        scale_table = sb.tile([P, T], U8, name="scale_table", align_bytes=64)
-        w2_raw = [sb.tile([P, 2, N], F32, name="w2_raw%d" % g, align_bytes=64) for g in range(2)]
-
-        nc.vector.memset(scale_table[:].bitcast(I32), 0)
-
-        w2_rows = w2.rearrange("(p j) c -> p j c", j=PACK)
-        nc.sync.dma_start(w2_raw[0][:], w2_rows[:, 0:2, :])
-        nc.sync.dma_start(offs_sb[:], offs)
-        nc.sync.dma_start(scale_table[0:P:8, :].bitcast(I32), x_scales[0].bitcast(I32))
-        nc.sync.dma_start(w2_raw[1][:], w2_rows[:, 2:4, :])
-        nc.sync.dma_start(word_table[:].bitcast(I32), x_words[0].rearrange("p n t -> p (n t)").bitcast(I32))
-        w1_rows = w1.rearrange("(p j) c -> p j c", j=PACK)
-        w1_early = sb.tile([P, 2, N], F32, name="w1_early", align_bytes=64)
-        nc.sync.dma_start(w1_early[:], w1_rows[:, 0:2, :])
+        scale_table = held.tile([P, T], U8, name="scale_table", align_bytes=64, offset=3072)
+        w2_raw = sb.tile([P, PACK, N], F32, name="w2_raw", align_bytes=64)
         x_codes = sb.tile([P, S], U32, name="x_codes", align_bytes=64)
         x_scale = sb.tile([P, S], U8, name="x_scale", align_bytes=64)
         picked_scales = sb.tile([P, S], U8, name="picked_scales", align_bytes=64)
+
+        def entries(offsets, lo, hi):
+            return offsets[:, lo // 16 : hi // 16]
+
+        nc.vector.memset(scale_table[:].bitcast(I32), 0)
         nc.vector.memset(x_scale[:].bitcast(I32), 0)
+        w2_rows = w2.rearrange("(p j) c -> p j c", j=PACK)
+        nc.sync.dma_start(w2_raw[:, 0:1, :], w2_rows[:, 0:1, :])
+        nc.sync.dma_start(offs_sb[:], offs)
+        nc.sync.dma_start(scale_table[0:P:8, :].bitcast(I32), x_scales[0].bitcast(I32))
+        nc.sync.dma_start(w2_raw[:, 1:4, :], w2_rows[:, 1:4, :])
+        nc.sync.dma_start(word_table[:].bitcast(I32), x_words[0].rearrange("p n t -> p (n t)").bitcast(I32))
+        nc.sync.dma_start(slot_sb[:], slot)
         nc.vector.tensor_copy(picked_scales[:], scale_table[:].indirect(offs_sb[:]))
         for r in range(4):
-            nc.sync.dma_start(x_scale[r:P:32, :].bitcast(I32), picked_scales[8 * r : P : 32, :].bitcast(I32))
-        w1_late = sb.tile([P, 2, N], F32, name="w1_late", tag="scale_table", align_bytes=64)
-        nc.sync.dma_start(w1_late[:], w1_rows[:, 2:4, :])
-        nc.sync.dma_start(slot_sb[:], slot)
-        cache_rows = cache.rearrange("(p t) c -> p t c", t=PACK)
+            queue = nc.scalar if r % 2 else nc.sync
+            queue.dma_start(x_scale[r:P:32, :].bitcast(I32), picked_scales[8 * r : P : 32, :].bitcast(I32))
+        w1_rows = w1.rearrange("(p j) c -> p j c", j=PACK)
+        w1_raw = []
+        for g in range(2):
+            w1_raw.append(held.tile([P, 2, N], F32, name="w1_raw%d" % g, align_bytes=64, offset=4096 * g))
+            nc.sync.dma_start(w1_raw[g][:], w1_rows[:, 2 * g : 2 * g + 2, :])
 
-        def quantize_weight(dealt, label):
+        def deal(dealt, raw, row, first, last):
+            nc.vector.tensor_copy(
+                dealt[:].rearrange("p (t m j) -> p m j t", t=PACK, j=PACK)[:, :, row : row + raw.shape[1], first:last],
+                raw[:].rearrange("p j (m t) -> p m j t", t=PACK)[:, :, :, first:last],
+            )
+
+        def quantize_weight(dealt, label, groups):
             codes = sb.tile([P, N], U32, name="%s_codes" % label, align_bytes=64)
             scales = sb.tile([P, N], U8, name="%s_scales" % label, align_bytes=64)
-            for u in range(2):
-                cols = slice(2 * P * u, 2 * P * (u + 1))
-                nc.vector.quantize_mx(out=codes[:, cols].bitcast(FP8X4), scales=scales[:, cols], in_=dealt[u])
+            for first, last in groups:
+                cols = slice(P * first, P * last)
+                nc.vector.quantize_mx(
+                    out=codes[:, cols].bitcast(FP8X4), scales=scales[:, cols], in_=dealt[:, N * first : N * last]
+                )
             return [(codes[:, t * P : (t + 1) * P], scales[:, t * P : (t + 1) * P]) for t in range(PACK)]
 
         w2_dealt = sb.tile([P, N * PACK], BF16, name="w2_dealt", align_bytes=64)
-        for g, copy in enumerate((nc.scalar.copy, nc.vector.tensor_copy)):
-            copy(
-                w2_dealt[:].rearrange("p (t m j) -> p m j t", t=PACK, j=PACK)[:, :, 2 * g : 2 * g + 2, :],
-                w2_raw[g][:].rearrange("p j (m t) -> p m j t", t=PACK),
+        for u in range(2):
+            deal(w2_dealt, w2_raw, 0, 2 * u, 2 * u + 2)
+        gate_w = quantize_weight(w2_dealt, "w2", ((0, 2), (2, 4)))
+
+        cache_rows = cache.rearrange("(p t) c -> p t c", t=PACK)
+        rows = [None] * PACK
+        for t, tag in zip((1, 0, 2, 3), ("w2_raw", "w2_dealt", "picked_scales", "word_table")):
+            rows[t] = sb.tile([P, U], F32, name="rows%d" % t, tag=tag, align_bytes=64)
+            nc.sync.dma_start(rows[t][:], cache_rows[:, t, :])
+
+        for lo, hi in ((0, LEAD), (LEAD, HALF), (HALF, S)):
+            nc.vector.tensor_copy(x_codes[:, lo:hi], word_table[:].indirect(entries(offs_sb, lo, hi)))
+
+        def bank(tag):
+            return psum.tile([P, S], F32, name=tag)
+
+        def multiply(acc, weights, lo, hi):
+            codes, scales = weights
+            nc.tensor.matmul_mx(
+                out=acc,
+                lhsT=codes.bitcast(FP8X4),
+                lhsT_scale=scales,
+                rhs=x_codes[:, lo:hi].bitcast(FP8X4),
+                rhs_scale=x_scale[:, lo:hi],
+                start=True,
+                stop=True,
             )
-        gate_w = quantize_weight([w2_dealt[:, :1024], w2_dealt[:, 1024:]], "w2")
+
+        gates = sb.tile([P, PACK * S], F32, name="gates", align_bytes=64)
+        early_gates = gates[:].rearrange("p (t k) -> p t k", t=PACK)[:, 0:3:2, :]
+        for h, pieces in enumerate((((0, LEAD), (LEAD, HALF)), ((HALF, S),))):
+            acc = bank("gate_half%d" % h)
+            for lo, hi in pieces:
+                for e, t in enumerate((1, 0)):
+                    multiply(acc[:, (e - h) * HALF + lo : (e - h) * HALF + hi], gate_w[t], lo, hi)
+            nc.scalar.activation(
+                early_gates[:, :, h * HALF : (h + 1) * HALF], acc[:].rearrange("p (e k) -> p e k", e=2), SIGMOID
+            )
+
+        def plane(tile, t, lo, hi):
+            return tile[:, PLANE[t] * S + lo : PLANE[t] * S + hi]
+
+        for t, hi in ((2, S), (3, HALF)):
+            acc = bank("gate%d" % t)
+            multiply(acc[:, :hi], gate_w[t], 0, hi)
+            nc.scalar.activation(plane(gates, t, 0, hi), acc[:, :hi], SIGMOID)
 
         w1_dealt = sb.tile([P, N * PACK], BF16, name="w1_dealt", align_bytes=64)
-        w1_target = w1_dealt[:].rearrange("p (t m j) -> p m j t", t=PACK, j=PACK)
-        rows = [None] * PACK
-        for t, tag in zip((1, 0, 3, 2), ("w2_raw1", "picked_scales", "word_table", "scale_table")):
-            rows[t] = sb.tile([P, U], F32, name="rows%d" % t, tag=tag, align_bytes=64)
-        for t in (1, 0, 3, 2):
-            nc.sync.dma_start(rows[t][:], cache_rows[:, t, :])
-        for h in range(2):
-            nc.vector.tensor_copy(
-                x_codes[:, h * HALF : (h + 1) * HALF],
-                word_table[:].indirect(offs_sb[:, h * HALF // 16 : (h + 1) * HALF // 16]),
-            )
-        nc.vector.tensor_copy(w1_target[:, :, 0:2, :], w1_early[:].rearrange("p j (m t) -> p m j t", t=PACK))
-
-        def product(weights, lo, hi):
-            acc = psum.tile([P, len(weights), hi - lo], F32, name="acc")
-            for e, (codes, scales) in enumerate(weights):
-                nc.tensor.matmul_mx(
-                    out=acc[:, e, :],
-                    lhsT=codes.bitcast(FP8X4),
-                    lhsT_scale=scales,
-                    rhs=x_codes[:, lo:hi].bitcast(FP8X4),
-                    rhs_scale=x_scale[:, lo:hi],
-                    start=True,
-                    stop=True,
-                )
-            return acc
-
-        gates = sb.tile([P, PACK, S], F32, name="gates", align_bytes=64)
-        for h in range(2):
-            lo, hi = h * HALF, (h + 1) * HALF
-            nc.scalar.activation(gates[:, 0:2, lo:hi], product(gate_w[0:2], lo, hi)[:], SIGMOID)
-        for t in (3, 2):
-            nc.scalar.activation(gates[:, t, :], product(gate_w[t : t + 1], 0, S)[:, 0, :], SIGMOID)
+        deal(w1_dealt, w1_raw[0], 0, 0, 4)
         for u in range(2):
-            nc.vector.tensor_copy(
-                w1_target[:, :, 2:4, 2 * u : 2 * u + 2],
-                w1_late[:].rearrange("p j (m t) -> p m j t", t=PACK)[:, :, :, 2 * u : 2 * u + 2],
-            )
-        value_w = quantize_weight([w1_dealt[:, :1024], w1_dealt[:, 1024:]], "w1")
+            deal(w1_dealt, w1_raw[1], 2, 2 * u, 2 * u + 2)
+        value_w = quantize_weight(w1_dealt, "w1", ((1, 2), (0, 1), (2, 4)))
 
-        early = sb.tile([P, 2, S], F32, name="early", align_bytes=64)
-        late = sb.tile([P, 2 * U], F32, name="late", align_bytes=64)
-        gated = [early[:], late[:, U:].rearrange("p (e k) -> p e k", e=2)]
-        for t in (1, 0, 3, 2):
-            acc = product(value_w[t : t + 1], 0, S)
+        gated = sb.tile([P, PACK * S], F32, name="gated", align_bytes=64)
+        acc = bank("lead")
+        multiply(acc[:, :HALF], value_w[1], 0, HALF)
+        nc.vector.tensor_tensor(plane(gated, 1, 0, HALF), acc[:, :HALF], plane(gates, 1, 0, HALF), MULT)
+        for t in (0, 2):
+            acc = bank("value%d" % t)
+            multiply(acc[:], value_w[t], 0, S)
+            nc.vector.tensor_tensor(plane(gated, t, 0, S), acc[:], plane(gates, t, 0, S), MULT)
             if t == 0:
-                nc.scalar.copy(gated[0][:, 0, :], acc[:, 0, :])
-            else:
-                nc.vector.tensor_tensor(gated[t // 2][:, t % 2, :], acc[:, 0, :], gates[:, t, :], MULT)
+                acc = bank("middle")
+                multiply(acc[:, :HALF], value_w[1], HALF, S)
+                multiply(acc[:, HALF:], value_w[3], 0, HALF)
+                nc.vector.tensor_tensor(gated[:, HALF : HALF + S], acc[:], gates[:, HALF : HALF + S], MULT)
+        last = bank("lead")
+        multiply(last[:, :HALF], gate_w[3], HALF, S)
+        multiply(last[:, HALF:], value_w[3], HALF, S)
+
+        def scalar_scatter(t, lo, hi):
+            nc.scalar.activation(rows[t][:].indirect(entries(slot_sb, lo, hi)), plane(gated, t, lo, hi), COPY)
+
+        def vector_scatter(t, lo, hi):
+            nc.vector.tensor_copy(rows[t][:].indirect(entries(slot_sb, lo, hi)), plane(gated, t, lo, hi))
 
         out_rows = out_0.rearrange("(p t) c -> p t c", t=PACK)
-        pairs = late[:].bitcast(BF16).rearrange("p (u c e) -> p u c e", u=2, e=2)
-        for u in range(2):
-            if u == 0:
-                nc.vector.tensor_tensor(rows[0][:].indirect(slot_sb[:]), gated[0][:, 0, :], gates[:, 0, :], MULT)
-            else:
-                nc.vector.tensor_copy(rows[2][:].indirect(slot_sb[:]), gated[1][:, 0, :])
-            for h in range(2):
-                nc.scalar.activation(
-                    rows[2 * u + 1][:].indirect(slot_sb[:, h * HALF // 16 : (h + 1) * HALF // 16]),
-                    gated[u][:, 1, h * HALF : (h + 1) * HALF],
-                    COPY,
-                )
-            for e in (1, 0):
-                nc.sync.dma_start(out_rows[:, 2 * u + e, :], rows[2 * u + e][:])
-        for e in (1, 0):
-            nc.gpsimd.tensor_scalar(pairs[:, 0, :, e], rows[e][:], 1.0, -0.0, MULT, ADD)
-        nc.vector.tensor_copy(pairs[:, 1, :SPLIT, 0], rows[2][:, :SPLIT])
-        for lo, hi in ((0, 256), (256, SPLIT)):
+        pair_words = sb.tile([P, 2 * U], F32, name="pair_words", align_bytes=64)
+        pairs = pair_words[:].bitcast(BF16).rearrange("p (u c e) -> p u c e", u=2, e=2)
+
+        scalar_scatter(1, 0, HALF)
+        nc.scalar.activation(plane(gates, 3, HALF, S), last[:, :HALF], SIGMOID)
+        scalar_scatter(1, HALF, S)
+        nc.sync.dma_start(out_rows[:, 1, :], rows[1][:])
+        nc.gpsimd.tensor_scalar(pairs[:, 0, :, 1], rows[1][:], 1.0, -0.0, MULT, ADD)
+
+        vector_scatter(0, 0, S)
+        nc.vector.tensor_tensor(plane(gated, 3, HALF, S), last[:, HALF:], plane(gates, 3, HALF, S), MULT)
+        nc.sync.dma_start(out_rows[:, 0, :], rows[0][:])
+        nc.gpsimd.tensor_scalar(pairs[:, 0, :, 0], rows[0][:], 1.0, -0.0, MULT, ADD)
+
+        scalar_scatter(2, 0, SHARED)
+        vector_scatter(2, SHARED, S)
+        nc.sync.dma_start(out_rows[:, 2, :], rows[2][:])
+        nc.vector.tensor_copy(pairs[:, 1, :, 0], rows[2][:])
+
+        scalar_scatter(3, 0, HALF)
+        scalar_scatter(3, HALF, S)
+        nc.sync.dma_start(out_rows[:, 3, :], rows[3][:])
+        for lo, hi in ROUNDS:
             nc.vector.tensor_copy(pairs[:, 1, lo:hi, 1], rows[3][:, lo:hi])
-        nc.scalar.copy(pairs[:, 1, SPLIT:, 1], rows[3][:, SPLIT:])
-        for lo, hi in ((SPLIT, 768), (768, U)):
-            nc.scalar.copy(pairs[:, 1, lo:hi, 0], rows[2][:, lo:hi])
 
         woven = sb.tile([P, U * 2], U32, name="woven", align_bytes=64)
         out_codes = sb.tile([P, U], U32, name="out_codes", align_bytes=64)
         out_scales = sb.tile([P, U // 2], U8, name="out_scales", align_bytes=64)
         words_hbm = out_1[0].rearrange("p n t -> p (n t)").bitcast(I32)
-        words = late[:].bitcast(U32).rearrange("p (u c) -> p c u", u=2)
+        words = pair_words[:].bitcast(U32).rearrange("p (u c) -> p c u", u=2)
         woven_words = woven[:].rearrange("p (c u) -> p c u", u=2)
-        for lo, hi in ((0, 256), (256, SPLIT)):
-            nc.vector.tensor_copy(woven_words[:, lo:hi, :].bitcast(I32), words[:, lo:hi, :].bitcast(I32))
-        for lo, hi in ((SPLIT, 768), (768, 896), (896, U)):
+        nc.vector.tensor_copy(woven_words[:, :OWN, :].bitcast(I32), words[:, :OWN, :].bitcast(I32))
+        for lo, hi in SCALAR_WEAVES:
             nc.scalar.copy(woven_words[:, lo:hi, :], words[:, lo:hi, :])
-        for lo, hi in zip(PIECES, PIECES[1:]):
+        for lo, hi in QUANTISED:
             nc.vector.quantize_mx(
                 out=out_codes[:, lo:hi].bitcast(FP8X4),
                 scales=out_scales[4 * (lo // S) :, lo % S : lo % S + hi - lo],
                 in_=woven[:, lo * 2 : hi * 2].bitcast(BF16),
             )
-            if hi in STORES:
-                first = STORES[STORES.index(hi) - 1]
-                nc.sync.dma_start(words_hbm[:, first:hi], out_codes[:, first:hi].bitcast(I32))
+            if (lo, hi) in STORED:
+                first, last = STORED[(lo, hi)]
+                nc.sync.dma_start(words_hbm[:, first:last], out_codes[:, first:last].bitcast(I32))
         for q in range(4):
             queue = nc.scalar if q % 2 else nc.sync
             queue.dma_start(

@@ -21,13 +21,11 @@ P = 128
 PACK = 4
 HALF = S // 2
 LEAD = 128
-PLANE = {1: 0, 3: 1, 0: 2, 2: 3}
-SHARED = 192
-OWN = 384
-ROUNDS = ((384, 640), (0, 384), (640, 1024))
-SCALAR_WEAVES = ((384, 640), (640, 896), (896, 1024))
-QUANTISED = ((384, 512), (0, 256), (256, 384), (512, 768), (768, 896), (896, 1024))
-STORED = {(0, 256): (0, 256), (256, 384): (256, 512), (512, 768): (512, 768), (896, 1024): (768, 1024)}
+REST = S - LEAD
+PLANE = {0: 0, 2: 1, 3: 2, 1: 3}
+SPLIT = 512
+PIECES = (0, 256, 512, 768, 896, 1024)
+STORES = (0, 512, 896, 1024)
 
 
 def tile_picked_zkvw_two_po_kernel(
@@ -93,11 +91,13 @@ def tile_picked_zkvw_two_po_kernel(
 
         cache_rows = cache.rearrange("(p t) c -> p t c", t=PACK)
         rows = [None] * PACK
-        for t, tag in zip((1, 0, 2, 3), ("w2_raw", "w2_dealt", "picked_scales", "word_table")):
+        for t, tag in zip((1, 0, 3), ("w2_raw", "w2_dealt", "word_table")):
             rows[t] = sb.tile([P, U], F32, name="rows%d" % t, tag=tag, align_bytes=64)
+        rows[2] = held.tile([P, U], F32, name="rows2", align_bytes=64, offset=0)
+        for t in (1, 0, 3, 2):
             nc.sync.dma_start(rows[t][:], cache_rows[:, t, :])
 
-        for lo, hi in ((0, LEAD), (LEAD, HALF), (HALF, S)):
+        for lo, hi in ((REST, S), (HALF, REST), (0, HALF)):
             nc.vector.tensor_copy(x_codes[:, lo:hi], word_table[:].indirect(entries(offs_sb, lo, hi)))
 
         def bank(tag):
@@ -116,23 +116,28 @@ def tile_picked_zkvw_two_po_kernel(
             )
 
         gates = sb.tile([P, PACK * S], F32, name="gates", align_bytes=64)
-        early_gates = gates[:].rearrange("p (t k) -> p t k", t=PACK)[:, 0:3:2, :]
-        for h, pieces in enumerate((((0, LEAD), (LEAD, HALF)), ((HALF, S),))):
-            acc = bank("gate_half%d" % h)
-            for lo, hi in pieces:
-                for e, t in enumerate((1, 0)):
-                    multiply(acc[:, (e - h) * HALF + lo : (e - h) * HALF + hi], gate_w[t], lo, hi)
-            nc.scalar.activation(
-                early_gates[:, :, h * HALF : (h + 1) * HALF], acc[:].rearrange("p (e k) -> p e k", e=2), SIGMOID
-            )
+        gate_planes = gates[:].rearrange("p (t k) -> p t k", t=PACK)
 
-        def plane(tile, t, lo, hi):
-            return tile[:, PLANE[t] * S + lo : PLANE[t] * S + hi]
+        def halves(acc):
+            return acc[:].rearrange("p (e k) -> p e k", e=2)
 
-        for t, hi in ((2, S), (3, HALF)):
-            acc = bank("gate%d" % t)
-            multiply(acc[:, :hi], gate_w[t], 0, hi)
-            nc.scalar.activation(plane(gates, t, 0, hi), acc[:, :hi], SIGMOID)
+        acc = bank("gate_a")
+        for lo, hi in ((REST, S), (HALF, REST)):
+            for e, t in ((1, 1), (0, 3)):
+                multiply(halves(acc)[:, e, lo - HALF : hi - HALF], gate_w[t], lo, hi)
+        nc.scalar.activation(gate_planes[:, 2:4, HALF:], halves(acc), SIGMOID)
+        acc = bank("gate_b")
+        for t in (1, 0):
+            multiply(halves(acc)[:, t, :], gate_w[t], 0, HALF)
+        nc.scalar.activation(gate_planes[:, 0:4:3, :HALF], halves(acc), SIGMOID)
+        acc = bank("gate_c")
+        multiply(acc[:, :HALF], gate_w[0], HALF, S)
+        multiply(acc[:, HALF:], gate_w[2], 0, HALF)
+        nc.scalar.activation(gates[:, HALF : HALF + S], acc[:], SIGMOID)
+        acc = bank("gate_d")
+        multiply(acc[:, :HALF], gate_w[2], HALF, S)
+        multiply(acc[:, HALF:], gate_w[3], 0, HALF)
+        nc.scalar.activation(gates[:, S + HALF : 2 * S + HALF], acc[:], SIGMOID)
 
         w1_dealt = sb.tile([P, N * PACK], BF16, name="w1_dealt", align_bytes=64)
         deal(w1_dealt, w1_raw[0], 0, 0, 4)
@@ -140,73 +145,75 @@ def tile_picked_zkvw_two_po_kernel(
             deal(w1_dealt, w1_raw[1], 2, 2 * u, 2 * u + 2)
         value_w = quantize_weight(w1_dealt, "w1", ((1, 2), (0, 1), (2, 4)))
 
-        gated = sb.tile([P, PACK * S], F32, name="gated", align_bytes=64)
-        acc = bank("lead")
-        multiply(acc[:, :HALF], value_w[1], 0, HALF)
-        nc.vector.tensor_tensor(plane(gated, 1, 0, HALF), acc[:, :HALF], plane(gates, 1, 0, HALF), MULT)
-        for t in (0, 2):
-            acc = bank("value%d" % t)
-            multiply(acc[:], value_w[t], 0, S)
-            nc.vector.tensor_tensor(plane(gated, t, 0, S), acc[:], plane(gates, t, 0, S), MULT)
-            if t == 0:
-                acc = bank("middle")
-                multiply(acc[:, :HALF], value_w[1], HALF, S)
-                multiply(acc[:, HALF:], value_w[3], 0, HALF)
-                nc.vector.tensor_tensor(gated[:, HALF : HALF + S], acc[:], gates[:, HALF : HALF + S], MULT)
-        last = bank("lead")
-        multiply(last[:, :HALF], gate_w[3], HALF, S)
-        multiply(last[:, HALF:], value_w[3], HALF, S)
+        work = sb.tile([P, U + PACK * S], F32, name="work", align_bytes=64)
+        gated = work[:, U:]
+
+        def gated_values(acc, pieces):
+            first = PLANE[pieces[0][0]] * S + pieces[0][1]
+            width = 0
+            for t, lo, hi in pieces:
+                multiply(acc[:, width : width + hi - lo], value_w[t], lo, hi)
+                width = width + hi - lo
+            nc.vector.tensor_tensor(
+                gated[:, first : first + width], acc[:, :width], gates[:, first : first + width], MULT
+            )
+
+        gated_values(bank("lead"), ((1, REST, S),))
+        gated_values(bank("gate_a"), ((0, 0, HALF),))
+        gated_values(bank("second"), ((1, 0, LEAD), (1, LEAD, REST)))
 
         def scalar_scatter(t, lo, hi):
-            nc.scalar.activation(rows[t][:].indirect(entries(slot_sb, lo, hi)), plane(gated, t, lo, hi), COPY)
+            values = gated[:, PLANE[t] * S + lo : PLANE[t] * S + hi]
+            nc.scalar.activation(rows[t][:].indirect(entries(slot_sb, lo, hi)), values, COPY)
 
         def vector_scatter(t, lo, hi):
-            nc.vector.tensor_copy(rows[t][:].indirect(entries(slot_sb, lo, hi)), plane(gated, t, lo, hi))
+            values = gated[:, PLANE[t] * S + lo : PLANE[t] * S + hi]
+            nc.vector.tensor_copy(rows[t][:].indirect(entries(slot_sb, lo, hi)), values)
 
         out_rows = out_0.rearrange("(p t) c -> p t c", t=PACK)
-        pair_words = sb.tile([P, 2 * U], F32, name="pair_words", align_bytes=64)
-        pairs = pair_words[:].bitcast(BF16).rearrange("p (u c e) -> p u c e", u=2, e=2)
+        words = work[:].bitcast(U32).rearrange("p (u c) -> p c u", u=2)
+        pairs = work[:].bitcast(BF16).rearrange("p (u c e) -> p u c e", u=2, e=2)
 
-        scalar_scatter(1, 0, HALF)
-        nc.scalar.activation(plane(gates, 3, HALF, S), last[:, :HALF], SIGMOID)
-        scalar_scatter(1, HALF, S)
-        nc.sync.dma_start(out_rows[:, 1, :], rows[1][:])
-        nc.gpsimd.tensor_scalar(pairs[:, 0, :, 1], rows[1][:], 1.0, -0.0, MULT, ADD)
-
-        vector_scatter(0, 0, S)
-        nc.vector.tensor_tensor(plane(gated, 3, HALF, S), last[:, HALF:], plane(gates, 3, HALF, S), MULT)
-        nc.sync.dma_start(out_rows[:, 0, :], rows[0][:])
-        nc.gpsimd.tensor_scalar(pairs[:, 0, :, 0], rows[0][:], 1.0, -0.0, MULT, ADD)
-
-        scalar_scatter(2, 0, SHARED)
-        vector_scatter(2, SHARED, S)
-        nc.sync.dma_start(out_rows[:, 2, :], rows[2][:])
-        nc.vector.tensor_copy(pairs[:, 1, :, 0], rows[2][:])
-
-        scalar_scatter(3, 0, HALF)
-        scalar_scatter(3, HALF, S)
-        nc.sync.dma_start(out_rows[:, 3, :], rows[3][:])
-        for lo, hi in ROUNDS:
-            nc.vector.tensor_copy(pairs[:, 1, lo:hi, 1], rows[3][:, lo:hi])
+        scalar_scatter(1, REST, S)
+        scalar_scatter(1, 0, REST)
+        vector_scatter(0, 0, HALF)
+        gated_values(bank("gate_b"), ((0, HALF, S),))
+        scalar_scatter(0, HALF, S)
+        for t in (1, 0):
+            nc.sync.dma_start(out_rows[:, t, :], rows[t][:])
+            nc.gpsimd.tensor_scalar(pairs[:, 0, :U, t], rows[t][:], 1.0, -0.0, MULT, ADD)
+        gated_values(bank("gate_c"), ((3, 0, S),))
+        gated_values(bank("gate_d"), ((2, 0, S),))
+        vector_scatter(3, REST, S)
+        scalar_scatter(3, 0, REST)
+        vector_scatter(2, 0, S)
+        for t in (3, 2):
+            nc.sync.dma_start(out_rows[:, t, :], rows[t][:])
+        nc.vector.tensor_copy(pairs[:, 1, :SPLIT, 1], rows[3][:, :SPLIT])
+        for lo, hi in ((0, 256), (256, SPLIT)):
+            nc.vector.tensor_copy(pairs[:, 1, lo:hi, 0], rows[2][:, lo:hi])
+        nc.scalar.copy(pairs[:, 1, SPLIT:U, 1], rows[3][:, SPLIT:])
+        for lo, hi in ((SPLIT, 768), (768, U)):
+            nc.scalar.copy(pairs[:, 1, lo:hi, 0], rows[2][:, lo:hi])
 
         woven = sb.tile([P, U * 2], U32, name="woven", align_bytes=64)
         out_codes = sb.tile([P, U], U32, name="out_codes", align_bytes=64)
         out_scales = sb.tile([P, U // 2], U8, name="out_scales", align_bytes=64)
         words_hbm = out_1[0].rearrange("p n t -> p (n t)").bitcast(I32)
-        words = pair_words[:].bitcast(U32).rearrange("p (u c) -> p c u", u=2)
         woven_words = woven[:].rearrange("p (c u) -> p c u", u=2)
-        nc.vector.tensor_copy(woven_words[:, :OWN, :].bitcast(I32), words[:, :OWN, :].bitcast(I32))
-        for lo, hi in SCALAR_WEAVES:
+        for lo, hi in ((0, 256), (256, SPLIT)):
+            nc.vector.tensor_copy(woven_words[:, lo:hi, :].bitcast(I32), words[:, lo:hi, :].bitcast(I32))
+        for lo, hi in ((SPLIT, 768), (768, 896), (896, U)):
             nc.scalar.copy(woven_words[:, lo:hi, :], words[:, lo:hi, :])
-        for lo, hi in QUANTISED:
+        for lo, hi in zip(PIECES, PIECES[1:]):
             nc.vector.quantize_mx(
                 out=out_codes[:, lo:hi].bitcast(FP8X4),
                 scales=out_scales[4 * (lo // S) :, lo % S : lo % S + hi - lo],
                 in_=woven[:, lo * 2 : hi * 2].bitcast(BF16),
             )
-            if (lo, hi) in STORED:
-                first, last = STORED[(lo, hi)]
-                nc.sync.dma_start(words_hbm[:, first:last], out_codes[:, first:last].bitcast(I32))
+            if hi in STORES:
+                first = STORES[STORES.index(hi) - 1]
+                nc.sync.dma_start(words_hbm[:, first:hi], out_codes[:, first:hi].bitcast(I32))
         for q in range(4):
             queue = nc.scalar if q % 2 else nc.sync
             queue.dma_start(

@@ -23,7 +23,7 @@ HALF = S // 2
 LEAD = 128
 REST = S - LEAD
 PLANE = {0: 0, 2: 1, 3: 2, 1: 3}
-SPLIT = 512
+SPLIT = 640
 PIECES = (0, 256, 512, 768, 896, 1024)
 STORES = (0, 512, 896, 1024)
 
@@ -193,7 +193,7 @@ def tile_picked_zkvw_two_po_kernel(
         for lo, hi in ((0, 256), (256, SPLIT)):
             nc.vector.tensor_copy(pairs[:, 1, lo:hi, 0], rows[2][:, lo:hi])
         nc.scalar.copy(pairs[:, 1, SPLIT:U, 1], rows[3][:, SPLIT:])
-        for lo, hi in ((SPLIT, 768), (768, U)):
+        for lo, hi in ((SPLIT, 832), (832, U)):
             nc.scalar.copy(pairs[:, 1, lo:hi, 0], rows[2][:, lo:hi])
 
         woven = sb.tile([P, U * 2], U32, name="woven", align_bytes=64)

@@ -23,7 +23,9 @@ HALF = S // 2
 LEAD = 128
 REST = S - LEAD
 PLANE = {0: 0, 2: 1, 3: 2, 1: 3}
-SPLIT = 640
+FIRST = 192
+LAST = 288
+SPLIT = 512
 PIECES = (0, 256, 512, 768, 896, 1024)
 STORES = (0, 512, 896, 1024)
 
@@ -74,20 +76,29 @@ def tile_picked_zkvw_two_po_kernel(
                 raw[:].rearrange("p j (m t) -> p m j t", t=PACK)[:, :, :, first:last],
             )
 
-        def quantize_weight(dealt, label, groups):
+        def mx_tiles(label):
             codes = sb.tile([P, N], U32, name="%s_codes" % label, align_bytes=64)
             scales = sb.tile([P, N], U8, name="%s_scales" % label, align_bytes=64)
-            for first, last in groups:
-                cols = slice(P * first, P * last)
-                nc.vector.quantize_mx(
-                    out=codes[:, cols].bitcast(FP8X4), scales=scales[:, cols], in_=dealt[:, N * first : N * last]
-                )
+            return codes, scales
+
+        def quantize_weight(tiles, dealt, first, last):
+            codes, scales = tiles
+            cols = slice(P * first, P * last)
+            nc.vector.quantize_mx(
+                out=codes[:, cols].bitcast(FP8X4), scales=scales[:, cols], in_=dealt[:, N * first : N * last]
+            )
+
+        def stationary(tiles):
+            codes, scales = tiles
             return [(codes[:, t * P : (t + 1) * P], scales[:, t * P : (t + 1) * P]) for t in range(PACK)]
 
         w2_dealt = sb.tile([P, N * PACK], BF16, name="w2_dealt", align_bytes=64)
         for u in range(2):
             deal(w2_dealt, w2_raw, 0, 2 * u, 2 * u + 2)
-        gate_w = quantize_weight(w2_dealt, "w2", ((0, 2), (2, 4)))
+        w2_mx = mx_tiles("w2")
+        for u in range(2):
+            quantize_weight(w2_mx, w2_dealt, 2 * u, 2 * u + 2)
+        gate_w = stationary(w2_mx)
 
         cache_rows = cache.rearrange("(p t) c -> p t c", t=PACK)
         rows = [None] * PACK
@@ -141,70 +152,78 @@ def tile_picked_zkvw_two_po_kernel(
 
         w1_dealt = sb.tile([P, N * PACK], BF16, name="w1_dealt", align_bytes=64)
         deal(w1_dealt, w1_raw[0], 0, 0, 4)
+        w1_mx = mx_tiles("w1")
         for u in range(2):
             deal(w1_dealt, w1_raw[1], 2, 2 * u, 2 * u + 2)
-        value_w = quantize_weight(w1_dealt, "w1", ((1, 2), (0, 1), (2, 4)))
+        for first, last in ((1, 2), (0, 1), (2, 4)):
+            quantize_weight(w1_mx, w1_dealt, first, last)
+        value_w = stationary(w1_mx)
 
-        work = sb.tile([P, U + PACK * S], F32, name="work", align_bytes=64)
-        gated = work[:, U:]
+        work = sb.tile([P, SPLIT + U + S], F32, name="work", align_bytes=64)
+        early = sb.tile([P, 2, S], F32, name="early", align_bytes=64)
+        gated = [early[:, 0, :], early[:, 1, :], work[:, :S], work[:, SPLIT + U :]]
 
-        def gated_values(acc, pieces):
-            first = PLANE[pieces[0][0]] * S + pieces[0][1]
-            width = 0
-            for t, lo, hi in pieces:
-                multiply(acc[:, width : width + hi - lo], value_w[t], lo, hi)
-                width = width + hi - lo
-            nc.vector.tensor_tensor(
-                gated[:, first : first + width], acc[:, :width], gates[:, first : first + width], MULT
-            )
+        def value_passes(acc, t, bounds):
+            for lo, hi in zip(bounds, bounds[1:]):
+                multiply(acc[:, lo - bounds[0] : hi - bounds[0]], value_w[t], lo, hi)
 
-        gated_values(bank("lead"), ((1, REST, S),))
-        gated_values(bank("gate_a"), ((0, 0, HALF),))
-        gated_values(bank("second"), ((1, 0, LEAD), (1, LEAD, REST)))
+        def apply_gate(acc, t, lo, hi):
+            cols = slice(PLANE[t] * S + lo, PLANE[t] * S + hi)
+            nc.vector.tensor_tensor(gated[t][:, lo:hi], acc[:, : hi - lo], gates[:, cols], MULT)
+
+        def gated_values(acc, t, bounds):
+            value_passes(acc, t, bounds)
+            apply_gate(acc, t, bounds[0], bounds[-1])
+
+        gated_values(bank("lead"), 1, (REST, S))
+        gated_values(bank("second"), 1, (0, LEAD, REST))
+        for t, tag in ((0, "gate_a"), (3, "gate_b"), (2, "gate_c")):
+            gated_values(bank(tag), t, (0, S))
 
         def scalar_scatter(t, lo, hi):
-            values = gated[:, PLANE[t] * S + lo : PLANE[t] * S + hi]
+            values = gated[t][:, lo:hi]
             nc.scalar.activation(rows[t][:].indirect(entries(slot_sb, lo, hi)), values, COPY)
 
         def vector_scatter(t, lo, hi):
-            values = gated[:, PLANE[t] * S + lo : PLANE[t] * S + hi]
+            values = gated[t][:, lo:hi]
             nc.vector.tensor_copy(rows[t][:].indirect(entries(slot_sb, lo, hi)), values)
 
         out_rows = out_0.rearrange("(p t) c -> p t c", t=PACK)
-        words = work[:].bitcast(U32).rearrange("p (u c) -> p c u", u=2)
-        pairs = work[:].bitcast(BF16).rearrange("p (u c e) -> p u c e", u=2, e=2)
+        pairs = work[:].bitcast(BF16).rearrange("p (c e) -> p c e", e=2)
+        early_pairs = pairs[:, SPLIT : SPLIT + U, :]
+        lower_pairs = pairs[:, :SPLIT, :]
+        upper_pairs = pairs[:, U : 2 * U, :]
 
         scalar_scatter(1, REST, S)
         scalar_scatter(1, 0, REST)
-        vector_scatter(0, 0, HALF)
-        gated_values(bank("gate_b"), ((0, HALF, S),))
-        scalar_scatter(0, HALF, S)
+        vector_scatter(0, 0, FIRST)
+        scalar_scatter(0, FIRST, S)
         for t in (1, 0):
             nc.sync.dma_start(out_rows[:, t, :], rows[t][:])
-            nc.gpsimd.tensor_scalar(pairs[:, 0, :U, t], rows[t][:], 1.0, -0.0, MULT, ADD)
-        gated_values(bank("gate_c"), ((3, 0, S),))
-        gated_values(bank("gate_d"), ((2, 0, S),))
-        vector_scatter(3, REST, S)
-        scalar_scatter(3, 0, REST)
+            nc.gpsimd.tensor_scalar(early_pairs[:, :, t], rows[t][:], 1.0, -0.0, MULT, ADD)
+        vector_scatter(3, LAST, S)
+        scalar_scatter(3, 0, LAST)
         vector_scatter(2, 0, S)
         for t in (3, 2):
             nc.sync.dma_start(out_rows[:, t, :], rows[t][:])
-        nc.vector.tensor_copy(pairs[:, 1, :SPLIT, 1], rows[3][:, :SPLIT])
+        nc.vector.tensor_copy(lower_pairs[:, :, 1], rows[3][:, :SPLIT])
         for lo, hi in ((0, 256), (256, SPLIT)):
-            nc.vector.tensor_copy(pairs[:, 1, lo:hi, 0], rows[2][:, lo:hi])
-        nc.scalar.copy(pairs[:, 1, SPLIT:U, 1], rows[3][:, SPLIT:])
-        for lo, hi in ((SPLIT, 832), (832, U)):
-            nc.scalar.copy(pairs[:, 1, lo:hi, 0], rows[2][:, lo:hi])
+            nc.vector.tensor_copy(lower_pairs[:, lo:hi, 0], rows[2][:, lo:hi])
+        nc.scalar.copy(upper_pairs[:, SPLIT:, 1], rows[3][:, SPLIT:])
+        for lo, hi in ((SPLIT, 768), (768, U)):
+            nc.scalar.copy(upper_pairs[:, lo:hi, 0], rows[2][:, lo:hi])
 
         woven = sb.tile([P, U * 2], U32, name="woven", align_bytes=64)
         out_codes = sb.tile([P, U], U32, name="out_codes", align_bytes=64)
         out_scales = sb.tile([P, U // 2], U8, name="out_scales", align_bytes=64)
         words_hbm = out_1[0].rearrange("p n t -> p (n t)").bitcast(I32)
         woven_words = woven[:].rearrange("p (c u) -> p c u", u=2)
+        lower = work[:, : 2 * SPLIT].bitcast(I32).rearrange("p (u c) -> p c u", u=2)[:, :, ::-1]
+        upper = work[:, 2 * SPLIT : 2 * U].bitcast(U32).rearrange("p (u c) -> p c u", u=2)
         for lo, hi in ((0, 256), (256, SPLIT)):
-            nc.vector.tensor_copy(woven_words[:, lo:hi, :].bitcast(I32), words[:, lo:hi, :].bitcast(I32))
+            nc.vector.tensor_copy(woven_words[:, lo:hi, :].bitcast(I32), lower[:, lo:hi, :])
         for lo, hi in ((SPLIT, 768), (768, 896), (896, U)):
-            nc.scalar.copy(woven_words[:, lo:hi, :], words[:, lo:hi, :])
+            nc.scalar.copy(woven_words[:, lo:hi, :], upper[:, lo - SPLIT : hi - SPLIT, :])
         for lo, hi in zip(PIECES, PIECES[1:]):
             nc.vector.quantize_mx(
                 out=out_codes[:, lo:hi].bitcast(FP8X4),

@@ -70,10 +70,11 @@ def tile_picked_zkvw_two_po_kernel(
             w1_raw.append(held.tile([P, 2, N], F32, name="w1_raw%d" % g, align_bytes=64, offset=4096 * g))
             nc.sync.dma_start(w1_raw[g][:], w1_rows[:, 2 * g : 2 * g + 2, :])
 
-        def deal(dealt, raw, row, first, last):
+        def deal(dealt, raw, row, first, last, lo=0, hi=P):
+            target = dealt[:].rearrange("p (t m j) -> p m j t", t=PACK, j=PACK)
             nc.vector.tensor_copy(
-                dealt[:].rearrange("p (t m j) -> p m j t", t=PACK, j=PACK)[:, :, row : row + raw.shape[1], first:last],
-                raw[:].rearrange("p j (m t) -> p m j t", t=PACK)[:, :, :, first:last],
+                target[:, lo:hi, row : row + raw.shape[1], first:last],
+                raw[:].rearrange("p j (m t) -> p m j t", t=PACK)[:, lo:hi, :, first:last],
             )
 
         def mx_tiles(label):
@@ -127,35 +128,28 @@ def tile_picked_zkvw_two_po_kernel(
             )
 
         gates = sb.tile([P, PACK * S], F32, name="gates", align_bytes=64)
-        gate_planes = gates[:].rearrange("p (t k) -> p t k", t=PACK)
-
-        def halves(acc):
-            return acc[:].rearrange("p (e k) -> p e k", e=2)
-
-        acc = bank("gate_a")
-        for lo, hi in ((REST, S), (HALF, REST)):
-            for e, t in ((1, 1), (0, 3)):
-                multiply(halves(acc)[:, e, lo - HALF : hi - HALF], gate_w[t], lo, hi)
-        nc.scalar.activation(gate_planes[:, 2:4, HALF:], halves(acc), SIGMOID)
-        acc = bank("gate_b")
-        for t in (1, 0):
-            multiply(halves(acc)[:, t, :], gate_w[t], 0, HALF)
-        nc.scalar.activation(gate_planes[:, 0:4:3, :HALF], halves(acc), SIGMOID)
-        acc = bank("gate_c")
-        multiply(acc[:, :HALF], gate_w[0], HALF, S)
-        multiply(acc[:, HALF:], gate_w[2], 0, HALF)
-        nc.scalar.activation(gates[:, HALF : HALF + S], acc[:], SIGMOID)
-        acc = bank("gate_d")
-        multiply(acc[:, :HALF], gate_w[2], HALF, S)
-        multiply(acc[:, HALF:], gate_w[3], 0, HALF)
-        nc.scalar.activation(gates[:, S + HALF : 2 * S + HALF], acc[:], SIGMOID)
+        for tag, pieces in (
+            ("gate_a", ((1, REST, S), (1, HALF, REST))),
+            ("gate_b", ((3, HALF, S), (1, 0, HALF))),
+            ("gate_c", ((0, 0, S),)),
+            ("gate_d", ((2, 0, S),)),
+            ("gate_e", ((3, 0, HALF),)),
+        ):
+            acc = bank(tag)
+            first = min(PLANE[t] * S + lo for t, lo, hi in pieces)
+            last = max(PLANE[t] * S + hi for t, lo, hi in pieces)
+            for t, lo, hi in pieces:
+                multiply(acc[:, PLANE[t] * S + lo - first : PLANE[t] * S + hi - first], gate_w[t], lo, hi)
+            nc.scalar.activation(gates[:, first:last], acc[:, : last - first], SIGMOID)
 
         w1_dealt = sb.tile([P, N * PACK], BF16, name="w1_dealt", align_bytes=64)
         deal(w1_dealt, w1_raw[0], 0, 0, 4)
         w1_mx = mx_tiles("w1")
-        for u in range(2):
-            deal(w1_dealt, w1_raw[1], 2, 2 * u, 2 * u + 2)
-        for first, last in ((1, 2), (0, 1), (2, 4)):
+        deal(w1_dealt, w1_raw[1], 2, 0, 2)
+        deal(w1_dealt, w1_raw[1], 2, 2, 4, 0, 80)
+        quantize_weight(w1_mx, w1_dealt, 1, 2)
+        deal(w1_dealt, w1_raw[1], 2, 2, 4, 80, P)
+        for first, last in ((0, 1), (2, 4)):
             quantize_weight(w1_mx, w1_dealt, first, last)
         value_w = stationary(w1_mx)
 
@@ -176,8 +170,17 @@ def tile_picked_zkvw_two_po_kernel(
             apply_gate(acc, t, bounds[0], bounds[-1])
 
         gated_values(bank("lead"), 1, (REST, S))
+        plain = sb.tile([P, S], F32, name="plain", align_bytes=64)
+
+        def gated_by_gpsimd(acc, lo, hi):
+            value_passes(acc, 0, (lo, hi))
+            nc.scalar.copy(plain[:, lo:hi], acc[:, : hi - lo])
+            nc.gpsimd.tensor_tensor(gated[0][:, lo:hi], plain[:, lo:hi], gates[:, lo:hi], MULT)
+
+        gated_by_gpsimd(bank("third"), 0, HALF)
         gated_values(bank("second"), 1, (0, LEAD, REST))
-        for t, tag in ((0, "gate_a"), (3, "gate_b"), (2, "gate_c")):
+        gated_values(bank("gate_a"), 0, (HALF, S))
+        for t, tag in ((3, "gate_b"), (2, "gate_c")):
             gated_values(bank(tag), t, (0, S))
 
         def scalar_scatter(t, lo, hi):

@@ -23,8 +23,8 @@ HALF = S // 2
 LEAD = 128
 REST = S - LEAD
 PLANE = {0: 0, 2: 1, 3: 2, 1: 3}
-FIRST = 192
-LAST = 288
+FIRST = 256
+LAST = 320
 SPLIT = 512
 PIECES = (0, 256, 512, 768, 896, 1024)
 STORES = (0, 512, 896, 1024)
@@ -146,11 +146,10 @@ def tile_picked_zkvw_two_po_kernel(
         deal(w1_dealt, w1_raw[0], 0, 0, 4)
         w1_mx = mx_tiles("w1")
         deal(w1_dealt, w1_raw[1], 2, 0, 2)
-        deal(w1_dealt, w1_raw[1], 2, 2, 4, 0, 80)
-        quantize_weight(w1_mx, w1_dealt, 1, 2)
-        deal(w1_dealt, w1_raw[1], 2, 2, 4, 80, P)
-        for first, last in ((0, 1), (2, 4)):
-            quantize_weight(w1_mx, w1_dealt, first, last)
+        deal(w1_dealt, w1_raw[1], 2, 2, 4, 0, 32)
+        for t in (1, 0):
+            quantize_weight(w1_mx, w1_dealt, t, t + 1)
+        deal(w1_dealt, w1_raw[1], 2, 2, 4, 32, P)
         value_w = stationary(w1_mx)
 
         work = sb.tile([P, SPLIT + U + S], F32, name="work", align_bytes=64)
@@ -170,18 +169,23 @@ def tile_picked_zkvw_two_po_kernel(
             apply_gate(acc, t, bounds[0], bounds[-1])
 
         gated_values(bank("lead"), 1, (REST, S))
-        plain = sb.tile([P, S], F32, name="plain", align_bytes=64)
+        quantize_weight(w1_mx, w1_dealt, 2, 4)
+        plain = sb.tile([P, 2, HALF], F32, name="plain", align_bytes=64)
 
-        def gated_by_gpsimd(acc, lo, hi):
-            value_passes(acc, 0, (lo, hi))
-            nc.scalar.copy(plain[:, lo:hi], acc[:, : hi - lo])
-            nc.gpsimd.tensor_tensor(gated[0][:, lo:hi], plain[:, lo:hi], gates[:, lo:hi], MULT)
+        def gated_by_gpsimd(acc, staged, t):
+            nc.scalar.copy(staged, acc[:, :HALF])
+            first = PLANE[t] * S
+            nc.gpsimd.tensor_tensor(gated[t][:, :HALF], staged, gates[:, first : first + HALF], MULT)
 
-        gated_by_gpsimd(bank("third"), 0, HALF)
-        gated_values(bank("second"), 1, (0, LEAD, REST))
+        acc = bank("third")
+        value_passes(acc, 0, (0, HALF))
+        gated_by_gpsimd(acc, plain[:, 0, :], 0)
         gated_values(bank("gate_a"), 0, (HALF, S))
-        for t, tag in ((3, "gate_b"), (2, "gate_c")):
-            gated_values(bank(tag), t, (0, S))
+        gated_values(bank("second"), 1, (0, LEAD, REST))
+        gated_values(bank("gate_b"), 3, (HALF, S))
+        gated_values(bank("gate_c"), 2, (0, S))
+        between = bank("lead")
+        value_passes(between, 3, (0, HALF))
 
         def scalar_scatter(t, lo, hi):
             values = gated[t][:, lo:hi]
@@ -198,6 +202,7 @@ def tile_picked_zkvw_two_po_kernel(
         upper_pairs = pairs[:, U : 2 * U, :]
 
         scalar_scatter(1, REST, S)
+        gated_by_gpsimd(between, plain[:, 1, :], 3)
         scalar_scatter(1, 0, REST)
         vector_scatter(0, 0, FIRST)
         scalar_scatter(0, FIRST, S)

@@ -223,7 +223,7 @@ def tile_picked_zkvw_two_po_kernel(
 
         woven = sb.tile([P, U * 2], U32, name="woven", align_bytes=64)
         out_codes = sb.tile([P, U], U32, name="out_codes", align_bytes=64)
-        out_scales = sb.tile([P, U // 2], U8, name="out_scales", align_bytes=64)
+        out_scales = sb.tile([P, U], U8, name="out_scales", align_bytes=64)
         words_hbm = out_1[0].rearrange("p n t -> p (n t)").bitcast(I32)
         woven_words = woven[:].rearrange("p (c u) -> p c u", u=2)
         lower = work[:, : 2 * SPLIT].bitcast(I32).rearrange("p (u c) -> p c u", u=2)[:, :, ::-1]
@@ -235,7 +235,7 @@ def tile_picked_zkvw_two_po_kernel(
         for lo, hi in zip(PIECES, PIECES[1:]):
             nc.vector.quantize_mx(
                 out=out_codes[:, lo:hi].bitcast(FP8X4),
-                scales=out_scales[4 * (lo // S) :, lo % S : lo % S + hi - lo],
+                scales=out_scales[:, lo:hi],
                 in_=woven[:, lo * 2 : hi * 2].bitcast(BF16),
             )
             if hi in STORES:
@@ -244,6 +244,6 @@ def tile_picked_zkvw_two_po_kernel(
         for q in range(4):
             queue = nc.scalar if q % 2 else nc.sync
             queue.dma_start(
-                out_2[0, 4 * q : 4 * q + 4, :].rearrange("r (h c) -> h r c", h=2).bitcast(I32),
-                out_scales[32 * q : 32 * q + 8, :].bitcast(I32),
+                out_2[0, q:16:4, :].bitcast(I32),
+                out_scales[q:P:32, :].bitcast(I32),
             )

@@ -41,12 +41,12 @@ def tile_picked_zkvw_two_po_kernel(
 
         offs_sb = sb.tile([P, S // 16], U16, name="offs_sb")
         slot_sb = sb.tile([P, S // 16], U16, name="slot_sb")
-        word_table = sb.tile([P, T], U32, name="word_table", align_bytes=64)
-        scale_table = held.tile([P, T], U8, name="scale_table", align_bytes=64, offset=3072)
-        w2_raw = sb.tile([P, PACK, N], F32, name="w2_raw", align_bytes=64)
-        x_codes = sb.tile([P, S], U32, name="x_codes", align_bytes=64)
-        x_scale = sb.tile([P, S], U8, name="x_scale", align_bytes=64)
-        picked_scales = sb.tile([P, S], U8, name="picked_scales", align_bytes=64)
+        word_table = sb.tile([P, T], U32, name="word_table", align_bytes=256)
+        scale_table = held.tile([P, T], U8, name="scale_table", align_bytes=256, offset=3072)
+        w2_raw = sb.tile([P, PACK, N], F32, name="w2_raw", align_bytes=256)
+        x_codes = sb.tile([P, S], U32, name="x_codes", align_bytes=256)
+        x_scale = sb.tile([P, S], U8, name="x_scale", align_bytes=256)
+        picked_scales = sb.tile([P, S], U8, name="picked_scales", align_bytes=256)
 
         def entries(offsets, lo, hi):
             return offsets[:, lo // 16 : hi // 16]
@@ -67,7 +67,7 @@ def tile_picked_zkvw_two_po_kernel(
         w1_rows = w1.rearrange("(p j) c -> p j c", j=PACK)
         w1_raw = []
         for g in range(2):
-            w1_raw.append(held.tile([P, 2, N], F32, name="w1_raw%d" % g, align_bytes=64, offset=4096 * g))
+            w1_raw.append(held.tile([P, 2, N], F32, name="w1_raw%d" % g, align_bytes=256, offset=4096 * g))
             nc.sync.dma_start(w1_raw[g][:], w1_rows[:, 2 * g : 2 * g + 2, :])
 
         def deal(dealt, raw, row, first, last, lo=0, hi=P):
@@ -78,8 +78,8 @@ def tile_picked_zkvw_two_po_kernel(
             )
 
         def mx_tiles(label):
-            codes = sb.tile([P, N], U32, name="%s_codes" % label, align_bytes=64)
-            scales = sb.tile([P, N], U8, name="%s_scales" % label, align_bytes=64)
+            codes = sb.tile([P, N], U32, name="%s_codes" % label, align_bytes=256)
+            scales = sb.tile([P, N], U8, name="%s_scales" % label, align_bytes=256)
             return codes, scales
 
         def quantize_weight(tiles, dealt, first, last):
@@ -93,7 +93,7 @@ def tile_picked_zkvw_two_po_kernel(
             codes, scales = tiles
             return [(codes[:, t * P : (t + 1) * P], scales[:, t * P : (t + 1) * P]) for t in range(PACK)]
 
-        w2_dealt = sb.tile([P, N * PACK], BF16, name="w2_dealt", align_bytes=64)
+        w2_dealt = sb.tile([P, N * PACK], BF16, name="w2_dealt", align_bytes=256)
         for u in range(2):
             deal(w2_dealt, w2_raw, 0, 2 * u, 2 * u + 2)
         w2_mx = mx_tiles("w2")
@@ -104,8 +104,8 @@ def tile_picked_zkvw_two_po_kernel(
         cache_rows = cache.rearrange("(p t) c -> p t c", t=PACK)
         rows = [None] * PACK
         for t, tag in zip((1, 0, 3), ("w2_raw", "w2_dealt", "word_table")):
-            rows[t] = sb.tile([P, U], F32, name="rows%d" % t, tag=tag, align_bytes=64)
-        rows[2] = held.tile([P, U], F32, name="rows2", align_bytes=64, offset=0)
+            rows[t] = sb.tile([P, U], F32, name="rows%d" % t, tag=tag, align_bytes=256)
+        rows[2] = held.tile([P, U], F32, name="rows2", align_bytes=256, offset=0)
         for t in (1, 0, 3, 2):
             nc.sync.dma_start(rows[t][:], cache_rows[:, t, :])
 
@@ -127,7 +127,7 @@ def tile_picked_zkvw_two_po_kernel(
                 stop=True,
             )
 
-        gates = sb.tile([P, PACK * S], F32, name="gates", align_bytes=64)
+        gates = sb.tile([P, PACK * S], F32, name="gates", align_bytes=256)
         for tag, pieces in (
             ("gate_a", ((1, REST, S), (1, HALF, REST))),
             ("gate_b", ((3, HALF, S), (1, 0, HALF))),
@@ -142,7 +142,7 @@ def tile_picked_zkvw_two_po_kernel(
                 multiply(acc[:, PLANE[t] * S + lo - first : PLANE[t] * S + hi - first], gate_w[t], lo, hi)
             nc.scalar.activation(gates[:, first:last], acc[:, : last - first], SIGMOID)
 
-        w1_dealt = sb.tile([P, N * PACK], BF16, name="w1_dealt", align_bytes=64)
+        w1_dealt = sb.tile([P, N * PACK], BF16, name="w1_dealt", align_bytes=256)
         deal(w1_dealt, w1_raw[0], 0, 0, 4)
         w1_mx = mx_tiles("w1")
         deal(w1_dealt, w1_raw[1], 2, 0, 2)
@@ -152,8 +152,8 @@ def tile_picked_zkvw_two_po_kernel(
         deal(w1_dealt, w1_raw[1], 2, 2, 4, 32, P)
         value_w = stationary(w1_mx)
 
-        work = sb.tile([P, SPLIT + U + S], F32, name="work", align_bytes=64)
-        early = sb.tile([P, 2, S], F32, name="early", align_bytes=64)
+        work = sb.tile([P, SPLIT + U + S], F32, name="work", align_bytes=256)
+        early = sb.tile([P, 2, S], F32, name="early", align_bytes=256)
         gated = [early[:, 0, :], early[:, 1, :], work[:, :S], work[:, SPLIT + U :]]
 
         def value_passes(acc, t, bounds):
@@ -170,7 +170,7 @@ def tile_picked_zkvw_two_po_kernel(
 
         gated_values(bank("lead"), 1, (REST, S))
         quantize_weight(w1_mx, w1_dealt, 2, 4)
-        plain = sb.tile([P, 2, HALF], F32, name="plain", align_bytes=64)
+        plain = sb.tile([P, 2, HALF], F32, name="plain", align_bytes=256)
 
         def gated_by_gpsimd(acc, staged, t):
             nc.scalar.copy(staged, acc[:, :HALF])
@@ -221,9 +221,9 @@ def tile_picked_zkvw_two_po_kernel(
         for lo, hi in ((SPLIT, 768), (768, U)):
             nc.scalar.copy(upper_pairs[:, lo:hi, 0], rows[2][:, lo:hi])
 
-        woven = sb.tile([P, U * 2], U32, name="woven", align_bytes=64)
-        out_codes = sb.tile([P, U], U32, name="out_codes", align_bytes=64)
-        out_scales = sb.tile([P, U], U8, name="out_scales", align_bytes=64)
+        woven = sb.tile([P, U * 2], U32, name="woven", align_bytes=256)
+        out_codes = sb.tile([P, U], U32, name="out_codes", align_bytes=256)
+        out_scales = sb.tile([P, U], U8, name="out_scales", align_bytes=256)
         words_hbm = out_1[0].rearrange("p n t -> p (n t)").bitcast(I32)
         woven_words = woven[:].rearrange("p (c u) -> p c u", u=2)
         lower = work[:, : 2 * SPLIT].bitcast(I32).rearrange("p (u c) -> p c u", u=2)[:, :, ::-1]

from contextlib import ExitStack

import concourse.mybir as mybir

K, T, S, N, U = 512, 2048, 512, 512, 1024
FLOPS = 2 * 2 * K * N * S

F32 = mybir.dt.float32
BF16 = mybir.dt.bfloat16
I32 = mybir.dt.int32
U32 = mybir.dt.uint32
U16 = mybir.dt.uint16
U8 = mybir.dt.uint8
FP8X4 = mybir.dt.float8_e4m3fn_x4
SIGMOID = mybir.ActivationFunctionType.Sigmoid
COPY = mybir.ActivationFunctionType.Copy
MULT = mybir.AluOpType.mult
ADD = mybir.AluOpType.add

P = 128
PACK = 4
HALF = S // 2
LEAD = 128
REST = S - LEAD
PLANE = {0: 0, 2: 1, 3: 2, 1: 3}
FIRST = 256
LAST = 320
SPLIT = 512
PIECES = (0, 256, 512, 768, 896, 1024)
STORES = (0, 512, 896, 1024)


def tile_picked_zkvw_two_po_kernel(
    tc, x_words, x_scales, cache, w1, w2, offs, slot, out_0, out_1, out_2
):
    nc = tc.nc
    with ExitStack() as ctx:
        sb = ctx.enter_context(tc.tile_pool(name="sb", bufs=1))
        held = ctx.enter_context(tc.tile_pool(name="held", bufs=1))
        psum = ctx.enter_context(tc.psum_pool(name="psum", bufs=1))

        offs_sb = sb.tile([P, S // 16], U16, name="offs_sb")
        slot_sb = sb.tile([P, S // 16], U16, name="slot_sb")
        word_table = sb.tile([P, T], U32, name="word_table", align_bytes=256)
        scale_table = held.tile([P, T], U8, name="scale_table", align_bytes=256, offset=3072)
        w2_raw = sb.tile([P, PACK, N], F32, name="w2_raw", align_bytes=256)
        x_codes = sb.tile([P, S], U32, name="x_codes", align_bytes=256)
        x_scale = sb.tile([P, S], U8, name="x_scale", align_bytes=256)
        picked_scales = sb.tile([P, S], U8, name="picked_scales", align_bytes=256)

        def entries(offsets, lo, hi):
            return offsets[:, lo // 16 : hi // 16]

        nc.vector.memset(scale_table[:].bitcast(I32), 0)
        nc.vector.memset(x_scale[:].bitcast(I32), 0)
        w2_rows = w2.rearrange("(p j) c -> p j c", j=PACK)
        nc.sync.dma_start(w2_raw[:, 0:1, :], w2_rows[:, 0:1, :])
        nc.sync.dma_start(offs_sb[:], offs)
        nc.sync.dma_start(scale_table[0:P:8, :].bitcast(I32), x_scales[0].bitcast(I32))
        nc.sync.dma_start(w2_raw[:, 1:4, :], w2_rows[:, 1:4, :])
        nc.sync.dma_start(word_table[:].bitcast(I32), x_words[0].rearrange("p n t -> p (n t)").bitcast(I32))
        nc.sync.dma_start(slot_sb[:], slot)
        nc.vector.tensor_copy(picked_scales[:], scale_table[:].indirect(offs_sb[:]))
        for r in range(4):
            queue = nc.scalar if r % 2 else nc.sync
            queue.dma_start(x_scale[r:P:32, :].bitcast(I32), picked_scales[8 * r : P : 32, :].bitcast(I32))
        w1_rows = w1.rearrange("(p j) c -> p j c", j=PACK)
        w1_raw = []
        for g in range(2):
            w1_raw.append(held.tile([P, 2, N], F32, name="w1_raw%d" % g, align_bytes=256, offset=4096 * g))
            nc.sync.dma_start(w1_raw[g][:], w1_rows[:, 2 * g : 2 * g + 2, :])

        def deal(dealt, raw, row, first, last, lo=0, hi=P):
            target = dealt[:].rearrange("p (t m j) -> p m j t", t=PACK, j=PACK)
            nc.vector.tensor_copy(
                target[:, lo:hi, row : row + raw.shape[1], first:last],
                raw[:].rearrange("p j (m t) -> p m j t", t=PACK)[:, lo:hi, :, first:last],
            )

        def mx_tiles(label):
            codes = sb.tile([P, N], U32, name="%s_codes" % label, align_bytes=256)
            scales = sb.tile([P, N], U8, name="%s_scales" % label, align_bytes=256)
            return codes, scales

        def quantize_weight(tiles, dealt, first, last):
            codes, scales = tiles
            cols = slice(P * first, P * last)
            nc.vector.quantize_mx(
                out=codes[:, cols].bitcast(FP8X4), scales=scales[:, cols], in_=dealt[:, N * first : N * last]
            )

        def stationary(tiles):
            codes, scales = tiles
            return [(codes[:, t * P : (t + 1) * P], scales[:, t * P : (t + 1) * P]) for t in range(PACK)]

        w2_dealt = sb.tile([P, N * PACK], BF16, name="w2_dealt", align_bytes=256)
        for u in range(2):
            deal(w2_dealt, w2_raw, 0, 2 * u, 2 * u + 2)
        w2_mx = mx_tiles("w2")
        for u in range(2):
            quantize_weight(w2_mx, w2_dealt, 2 * u, 2 * u + 2)
        gate_w = stationary(w2_mx)

        cache_rows = cache.rearrange("(p t) c -> p t c", t=PACK)
        rows = [None] * PACK
        for t, tag in zip((1, 0, 3), ("w2_raw", "w2_dealt", "word_table")):
            rows[t] = sb.tile([P, U], F32, name="rows%d" % t, tag=tag, align_bytes=256)
        rows[2] = held.tile([P, U], F32, name="rows2", align_bytes=256, offset=0)
        for t in (1, 0, 3, 2):
            nc.sync.dma_start(rows[t][:], cache_rows[:, t, :])

        for lo, hi in ((REST, S), (HALF, REST), (0, HALF)):
            nc.vector.tensor_copy(x_codes[:, lo:hi], word_table[:].indirect(entries(offs_sb, lo, hi)))

        def bank(tag):
            return psum.tile([P, S], F32, name=tag)

        def multiply(acc, weights, lo, hi):
            codes, scales = weights
            nc.tensor.matmul_mx(
                out=acc,
                lhsT=codes.bitcast(FP8X4),
                lhsT_scale=scales,
                rhs=x_codes[:, lo:hi].bitcast(FP8X4),
                rhs_scale=x_scale[:, lo:hi],
                start=True,
                stop=True,
            )

        gates = sb.tile([P, PACK * S], F32, name="gates", align_bytes=256)
        for tag, pieces in (
            ("gate_a", ((1, REST, S), (1, HALF, REST))),
            ("gate_b", ((3, HALF, S), (1, 0, HALF))),
            ("gate_c", ((0, 0, S),)),
            ("gate_d", ((2, 0, S),)),
            ("gate_e", ((3, 0, HALF),)),
        ):
            acc = bank(tag)
            first = min(PLANE[t] * S + lo for t, lo, hi in pieces)
            last = max(PLANE[t] * S + hi for t, lo, hi in pieces)
            for t, lo, hi in pieces:
                multiply(acc[:, PLANE[t] * S + lo - first : PLANE[t] * S + hi - first], gate_w[t], lo, hi)
            nc.scalar.activation(gates[:, first:last], acc[:, : last - first], SIGMOID)

        w1_dealt = sb.tile([P, N * PACK], BF16, name="w1_dealt", align_bytes=256)
        deal(w1_dealt, w1_raw[0], 0, 0, 4)
        w1_mx = mx_tiles("w1")
        deal(w1_dealt, w1_raw[1], 2, 0, 2)
        deal(w1_dealt, w1_raw[1], 2, 2, 4, 0, 32)
        for t in (1, 0):
            quantize_weight(w1_mx, w1_dealt, t, t + 1)
        deal(w1_dealt, w1_raw[1], 2, 2, 4, 32, P)
        value_w = stationary(w1_mx)

        work = sb.tile([P, SPLIT + U + S], F32, name="work", align_bytes=256)
        early = sb.tile([P, 2, S], F32, name="early", align_bytes=256)
        gated = [early[:, 0, :], early[:, 1, :], work[:, :S], work[:, SPLIT + U :]]

        def value_passes(acc, t, bounds):
            for lo, hi in zip(bounds, bounds[1:]):
                multiply(acc[:, lo - bounds[0] : hi - bounds[0]], value_w[t], lo, hi)

        def apply_gate(acc, t, lo, hi):
            cols = slice(PLANE[t] * S + lo, PLANE[t] * S + hi)
            nc.vector.tensor_tensor(gated[t][:, lo:hi], acc[:, : hi - lo], gates[:, cols], MULT)

        def gated_values(acc, t, bounds):
            value_passes(acc, t, bounds)
            apply_gate(acc, t, bounds[0], bounds[-1])

        gated_values(bank("lead"), 1, (REST, S))
        quantize_weight(w1_mx, w1_dealt, 2, 4)
        plain = sb.tile([P, 2, HALF], F32, name="plain", align_bytes=256)

        def gated_by_gpsimd(acc, staged, t):
            nc.scalar.copy(staged, acc[:, :HALF])
            first = PLANE[t] * S
            nc.gpsimd.tensor_tensor(gated[t][:, :HALF], staged, gates[:, first : first + HALF], MULT)

        acc = bank("third")
        value_passes(acc, 0, (0, HALF))
        gated_by_gpsimd(acc, plain[:, 0, :], 0)
        gated_values(bank("gate_a"), 0, (HALF, S))
        gated_values(bank("second"), 1, (0, LEAD, REST))
        gated_values(bank("gate_b"), 3, (HALF, S))
        gated_values(bank("gate_c"), 2, (0, S))
        between = bank("lead")
        value_passes(between, 3, (0, HALF))

        def scalar_scatter(t, lo, hi):
            values = gated[t][:, lo:hi]
            nc.scalar.activation(rows[t][:].indirect(entries(slot_sb, lo, hi)), values, COPY)

        def vector_scatter(t, lo, hi):
            values = gated[t][:, lo:hi]
            nc.vector.tensor_copy(rows[t][:].indirect(entries(slot_sb, lo, hi)), values)

        out_rows = out_0.rearrange("(p t) c -> p t c", t=PACK)
        pairs = work[:].bitcast(BF16).rearrange("p (c e) -> p c e", e=2)
        early_pairs = pairs[:, SPLIT : SPLIT + U, :]
        lower_pairs = pairs[:, :SPLIT, :]
        upper_pairs = pairs[:, U : 2 * U, :]

        scalar_scatter(1, REST, S)
        gated_by_gpsimd(between, plain[:, 1, :], 3)
        scalar_scatter(1, 0, REST)
        vector_scatter(0, 0, FIRST)
        scalar_scatter(0, FIRST, S)
        for t in (1, 0):
            nc.sync.dma_start(out_rows[:, t, :], rows[t][:])
            nc.gpsimd.tensor_scalar(early_pairs[:, :, t], rows[t][:], 1.0, -0.0, MULT, ADD)
        vector_scatter(3, LAST, S)
        scalar_scatter(3, 0, LAST)
        vector_scatter(2, 0, S)
        for t in (3, 2):
            nc.sync.dma_start(out_rows[:, t, :], rows[t][:])
        nc.vector.tensor_copy(lower_pairs[:, :, 1], rows[3][:, :SPLIT])
        for lo, hi in ((0, 256), (256, SPLIT)):
            nc.vector.tensor_copy(lower_pairs[:, lo:hi, 0], rows[2][:, lo:hi])
        nc.scalar.copy(upper_pairs[:, SPLIT:, 1], rows[3][:, SPLIT:])
        for lo, hi in ((SPLIT, 768), (768, U)):
            nc.scalar.copy(upper_pairs[:, lo:hi, 0], rows[2][:, lo:hi])

        woven = sb.tile([P, U * 2], U32, name="woven", align_bytes=256)
        out_codes = sb.tile([P, U], U32, name="out_codes", align_bytes=256)
        out_scales = sb.tile([P, U], U8, name="out_scales", align_bytes=256)
        words_hbm = out_1[0].rearrange("p n t -> p (n t)").bitcast(I32)
        woven_words = woven[:].rearrange("p (c u) -> p c u", u=2)
        lower = work[:, : 2 * SPLIT].bitcast(I32).rearrange("p (u c) -> p c u", u=2)[:, :, ::-1]
        upper = work[:, 2 * SPLIT : 2 * U].bitcast(U32).rearrange("p (u c) -> p c u", u=2)
        for lo, hi in ((0, 256), (256, SPLIT)):
            nc.vector.tensor_copy(woven_words[:, lo:hi, :].bitcast(I32), lower[:, lo:hi, :])
        for lo, hi in ((SPLIT, 768), (768, 896), (896, U)):
            nc.scalar.copy(woven_words[:, lo:hi, :], upper[:, lo - SPLIT : hi - SPLIT, :])
        for lo, hi in zip(PIECES, PIECES[1:]):
            nc.vector.quantize_mx(
                out=out_codes[:, lo:hi].bitcast(FP8X4),
                scales=out_scales[:, lo:hi],
                in_=woven[:, lo * 2 : hi * 2].bitcast(BF16),
            )
            if hi in STORES:
                first = STORES[STORES.index(hi) - 1]
                nc.sync.dma_start(words_hbm[:, first:hi], out_codes[:, first:hi].bitcast(I32))
        for q in range(4):
            queue = nc.scalar if q % 2 else nc.sync
            queue.dma_start(
                out_2[0, q:16:4, :].bitcast(I32),
                out_scales[q:P:32, :].bitcast(I32),
            )
